import numpy as np, ml_dtypes
CORES = [66,74,82,90,194,202,210,218]
N = 8
BF = ml_dtypes.bfloat16
W, L, B, CAP, C, S, RO = 2048, 256, 8, 64, 8, 32, 4
def work(rng, *shape):
    return B * rng.integers(0, L, shape) + rng.integers(0, RO, shape)
def land(rng, *shape):
    return S * rng.integers(0, CAP, shape) + RO + rng.integers(0, RO, shape)
def parts(rng):
    X = rng.integers(0, 256, (N, 8, 16, W)); R = rng.integers(0, W, (N, 8, 16, W)); R = np.where(rng.random(R.shape) < 0.5, R[:, :, :1], R)
    z = rng.random((N, 8, W)); A = np.where(z < 0.3, work(rng, N, 8, W), np.where(z < 0.5, land(rng, N, 8, W), rng.integers(0, W, (N, 8, W))))
    return X, R, A, rng.integers(0, 256, (N, 8, 16)), rng.integers(1000, 1250, (N, 8, 1)) + rng.integers(0, 200, (N, 8, 16))
def pack(X, R, A, w, th):
    return {"xc": np.ascontiguousarray(X.reshape(N, 128, W)).astype(np.float32).astype(BF), "rf": np.ascontiguousarray(R.reshape(N, 128, W)).astype(np.int32),
            "an": np.ascontiguousarray(A).astype(np.int32), "w": w.reshape(N, 128, 1).astype(np.int32), "th": th.reshape(N, 128, 1).astype(np.int32)}
def setup_inputs(rng):
    return pack(*parts(rng))
def setup_inputs_copies(rng):
    X, R, A, w, th = parts(rng); x = np.arange(W)
    R[:, 1::4] = np.repeat(R[:, 1::4, :1], 16, axis=2)
    R[:, 2::4, 1:] = (R[:, 2::4, :1] + rng.integers(1, W, (N, 2, 15, W))) & (W - 1)
    A[:, ::2] = (x - B) & (W - 1)
    A[:, 1::2] = np.where(rng.random((N, 4, W)) < 0.5, land(rng, N, 4, W), work(rng, N, 4, W))
    th = rng.choice(np.array([1100, 1300, 1500]), (N, 8, 1)) + rng.integers(0, 200, (N, 8, 16))
    return pack(X, R, A, w, th)
def setup_inputs_corners(rng):
    X, R, A, w, th = parts(rng); kk = np.arange(16).reshape(1, 1, 16, 1); x = np.arange(W); heads = B * np.arange(L); off = x & (B - 1)
    X = rng.integers(0, 4, (N, 8, 16, W)); R = rng.integers(0, W, (N, 8, 16, W))
    first = R[:, :, :1]; first = np.where((first & (B - 1)) == 0, first ^ 1, first)
    R = np.where((rng.random(R.shape) < 0.5) | (kk == 0), first, R)
    R = np.where(((R + 613 * kk) & (B - 1)) == 0, R ^ 1, R)
    th = rng.integers(49, 101, (N, 8, 16)); slow = []
    for q in range(N):
        for g in range(8):
            k = int(rng.choice(np.array([0, 1, CAP - 1, CAP, CAP + 1, L])))
            if q == 0: k = (CAP, CAP + 1, L, CAP - 1, 1, 0, CAP, CAP + 1)[g]
            if q == 1: k = (CAP, CAP - 1, 1, 0, 0, 0, 0, 256 - 2 * CAP)[g]
            if q == 2: k = 31 + int(g < 7)
            if q == N - 1 and g == 7: k = CAP
            o = rng.permutation(L)
            if g == 7 and k > 0:
                i = int(np.flatnonzero(o < k)[-1]); o[[i, L - 1]] = o[[L - 1, i]]
            go = o < k; h = np.where(go, 0, rng.integers(100, 256, (16, L))); near = rng.integers(10, 13, (16, L))
            if q == 1: h = np.where(~go & (rng.random(L) < 0.5), near, h)
            if q == 2:
                h = np.where(o < 56, 0, np.where(o < 186, near, h)); slow.append(heads[(o >= k) & (o < 186)])
            X[q, g][:, heads] = h
    w[:, 0::4] = 255; w[:, 1::4] = 0; w[1:3] = 0
    A[:, 0] = x; A[:, 1] = (W - 1) * rng.integers(0, 2, (N, W)); A[:, 2] = (x + 1) & (W - 1); A[:, 3] = (x - B) & (W - 1); A[:, 5] = (x - 1) & (W - 1)
    A[:, 6] = np.where(rng.random((N, W)) < 0.5, x, W - 1 - x)
    X[2][:, :, off == 1] = rng.integers(100, 256, (8, 16, L))
    to = B * rng.integers(0, L, (8, 16, W)) + np.where(off == 2, 1, rng.integers(2, B, (8, 16, W)))
    R[2] = (to - 613 * kk[0]) & (W - 1)
    A[2] = B * rng.integers(0, L, (8, W)) + 3
    A[2][:, 2 * B * np.arange(L // 2) + 2] = 2 * B * rng.integers(0, L // 2, (8, L // 2)) + B + 2
    for g in range(8): A[2, g, slow[g]] = 2 * B * rng.integers(0, L // 2, len(slow[g])) + 2
    return pack(X, R, A, w, th)
def setup_inputs_ends(rng):
    kind = rng.integers(0, 3, (N, 8, 1, W)); X = 255 * np.where(kind == 2, rng.integers(0, 2, (N, 8, 16, W)), kind)
    R = (W - 1) * rng.integers(0, 2, (N, 8, 16, W)); A = (W - 1) * rng.integers(0, 2, (N, 8, W))
    z = rng.random((N, 8, W)); A = np.where(z < 0.12, work(rng, N, 8, W), np.where(z < 0.25, land(rng, N, 8, W), A))
    w = 255 * rng.integers(0, 2, (N, 8, 16)); th = np.zeros((N, 8, 16), np.int64)
    for q in range(N):
        many = np.append(rng.permutation(np.array([C, C - 1, C - 2, C + 1, C - 1, C, C - 1])), C)
        i = int(np.flatnonzero(many == C)[0]); many[[i, 6]] = many[[6, i]]
        for g in range(8): th[q, g, rng.permutation(16)[:many[g]]] = 4080
    w[:, 7] = 255; w[:, 6] = 0; w[:, 6, 0] = 255; w[:, 6, 1] = 1
    for x in (0, W - B):
        X[:, 7, :, x] = 255; A[:, 7, x] = 0
    X[:, 6, 0, W - B] = 16; X[:, 6, 1, W - B] = 15; A[:, 6, W - B] = W - 1; R[:, 6, 0, W - B] = 0
    X[:, 6, 0, 0] = 15; X[:, 6, 1, 0] = 250; A[:, 6, 0] = W - 2; R[:, 6, 0, 0] = 0
    R[:, 6, :, W - 1] = W - 1
    R[:, 6, :, W - 2] = W - 3
    R[:, 7, 0, 0] = W - 1; R[:, 7, 14:, 0] = 0
    X[:, 7, :, (613 * 15) & (W - 1)] = 0; X[:, 7, :, (613 * 14) & (W - 1)] = 255
    return pack(X, R, A, w, th)
def setup_inputs_spread(rng):
    X = (rng.random((N, 8, 16, W)) * np.exp2(rng.integers(0, 9, (N, 8, 1, W)))).astype(np.int64)
    p = rng.choice(np.array([1, 2, 4]), (N, 8, 16, 1)); R = np.minimum((W * rng.random((N, 8, 16, W)) ** p).astype(np.int64), W - 1)
    R = np.where(rng.random(R.shape) < rng.random((N, 8, 1, W)), R[:, :, :1], R)
    p = rng.choice(np.array([1, 2, 4]), (N, 8, 1)); A = np.minimum((W * rng.random((N, 8, W)) ** p).astype(np.int64), W - 1)
    w = np.minimum(np.exp2(8 * rng.random((N, 8, 16))).astype(np.int64), 255) * (rng.random((N, 8, 16)) > 0.1)
    p = rng.choice(np.array([1, 2, 4, 8]), (N, 8, 1)); th = np.minimum((4081 * rng.random((N, 8, 16)) ** p).astype(np.int64), 4080)
    return pack(X, R, A, w, th)
def setup_inputs_ties(rng):
    X, R, A, w, th = parts(rng)
    pool = rng.integers(0, 256, (N, 8, 16, 6)); X = np.take_along_axis(pool, rng.integers(0, 6, (N, 8, 1, W)), 3)
    i = rng.integers(0, 6, (N, 8, 1, 16)); j = rng.integers(0, 6, (N, 8, 1, 16))
    d = np.add.reduce(np.abs(np.take_along_axis(pool, i, 3) - np.take_along_axis(pool, j, 3)), axis=2)
    return pack(X, R, A, w, np.minimum(d + rng.integers(0, 2, d.shape), 4080))
def check_inputs(d):
    bad = []
    for k, lo, hi in (("xc", 0, 255), ("rf", 0, W - 1), ("an", 0, W - 1), ("w", 0, 255), ("th", 0, 4080)):
        a = np.asarray(d[k]).astype(np.float64)
        if not (np.min(a) >= lo and np.max(a) <= hi): bad.append("range of " + k)
        elif np.any(a != np.floor(a)): bad.append("whole numbers in " + k)
    return bad
def cols(T, ix):
    return np.take_along_axis(T, ix[:, :, None, :], 3)
def dist(X, q, u, m):
    kk = np.arange(16).reshape(1, 1, 16, 1); s = ((m * u >> 5) + m + 613 * kk) & (W - 1)
    x = cols(X, s.reshape(N, 8, 16 * L)).reshape(N, 8, 16, 16, L)
    return np.add.reduce(np.abs(x - q[:, :, :, None, :]), axis=2).astype(np.int64)
def reference(xc, rf, an, w, th):
    X = xc.astype(np.float32).astype(np.int32).reshape(N, 8, 16, W); R = rf.astype(np.int64).reshape(N, 8, 16, W); A = an.astype(np.int64)
    ww = w.astype(np.int64).reshape(N, 8, 16, 1); tt = th.astype(np.int64).reshape(N, 8, 16, 1)
    v = np.zeros((N, 8, 1), np.int64) + B * np.arange(L); a = np.take_along_axis(A, v, 2); b = np.zeros((N, 1, 1, 1), np.int64)
    for t in range(RO):
        q = cols(X, v); u = np.add.reduce(ww * q, axis=2, keepdims=True) & 4095
        e = cols(R, a); own = np.take_along_axis(R[:, :, 0], v, 2)[:, :, None, :]
        n = np.where(e == e[:, :, :1], own, e)
        d, d2 = dist(X, q, u, e), dist(X, q, u, n)
        f = np.where(d2 < d, n, e); f[:, :, 0] = own[:, :, 0]
        fit = (np.add.reduce((np.minimum(d, d2) < tt + b).astype(np.int64), axis=2) >= C).astype(np.int64)
        b = (np.add.reduce(fit, axis=(1, 2)) & 255).reshape(N, 1, 1, 1)
        after = np.where(fit == 1, np.take_along_axis(A, v + 1, 2), np.take_along_axis(A, a, 2))
        r, g, i = np.nonzero(fit)
        R[r, g, :, v[r, g, i]] = f[r, g, :, i]; A[r, g, v[r, g, i]] = a[r, g, i]
        before = np.add.accumulate(fit, axis=2) - fit
        r, g, i = np.nonzero((fit == 1) & (before < CAP))
        R[(r + 1 + t % (N - 1)) % N, g, :, S * before[r, g, i] + RO + t] = f[r, g, :, i]
        v = v + fit; a = after
    o = R.reshape(N, 8, 16, L, B); o = o[..., :RO // 2] + 4096 * o[..., RO // 2:RO]
    h = R.reshape(N, 8, 16, CAP, S)[..., RO:2 * RO]
    return {"yr": o.reshape(N, 128, L * (RO // 2)).astype(np.float32), "yh": h.reshape(N, 128, CAP * RO).astype(np.float32),
            "yan": A.reshape(N, 8, L, B)[..., :RO].reshape(N, 8, L * RO).astype(np.float32), "yv": v.astype(np.float32), "ya": a.astype(np.float32)}

@@ -1,0 +1,497 @@
+from concourse.mybir import AluOpType as OP, ActivationFunctionType as AF, AxisListType
+
+TW = 2048
+DUMP = 3072
+SCRATCH = {}
+for _n, _w, _d in (
+    ("X2", 4096, "bfloat16"), ("R", 5120, "int32"), ("AA", 5120, "float32"), ("OWB", 2048, "float32"),
+    ("OWN", 1024, "float32"), ("U", 1024, "float32"), ("KN", 1024, "float32"), ("QS", 1024, "bfloat16"),
+    ("IOT", 2048, "float32"), ("SXF", 4096, "float32"), ("SXS", 2048, "float32"), ("MX", 4096, "bfloat16"),
+    ("QX", 2048, "bfloat16"), ("XG", 4096, "bfloat16"), ("DD", 4096, "bfloat16"), ("AD", 4096, "bfloat16"),
+    ("E", 2048, "bfloat16"), ("q", 256, "bfloat16"), ("u", 256, "float32"), ("kn", 256, "float32"),
+    ("ow", 256, "float32"), ("aB", 256, "float32"), ("AB", 512, "float32"), ("e", 256, "float32"),
+    ("prod", 256, "int32"), ("pl", 256, "int32"), ("pl16", 256, "uint16"), ("eqs", 256, "float32"),
+    ("xk", 256, "float32"), ("m", 256, "int32"), ("hit", 256, "bfloat16"), ("F", 264, "int32"),
+    ("fitb", 256, "float32"), ("cum", 256, "float32"), ("junk", 256, "float32"), ("acc", 4, "float32"),
+    ("inv16", 8, "uint16"), ("QT", 128, "bfloat16"), ("wsx", 256, "float32"),
+    ("fit", 16, "float32"), ("nf", 16, "float32"), ("f256", 16, "float32"), ("Aw", 32, "float32"), ("dA", 16, "float32"),
+    ("tA", 16, "float32"), ("aw", 16, "float32"), ("vtw", 16, "float32"), ("vw", 16, "float32"), ("vsw", 16, "float32"),
+    ("AL", 32, "uint16"), ("VT16", 16, "uint16"), ("VS16", 16, "uint16"),
+    ("bsum", 1, "float32"), ("bI", 2, "int32"), ("th4", 1, "float32"), ("thb", 1, "float32"),
+    ("thI", 1, "int32"), ("wI", 1, "int32"), ("wF", 1, "float32"),
+    ("pI", 1, "int32"), ("pF", 1, "float32"), ("qI", 1, "int32"), ("q16", 1, "float32"), ("c15", 1, "float32"),
+    ("rI", 1, "int32"), ("rF", 1, "float32"), ("hI", 1, "int32"), ("m1", 1, "float32"), ("m0", 1, "float32"),
+    ("isz", 1, "float32"), ("inz", 1, "float32"), ("kI", 1, "int32"), ("kJ", 1, "int32"), ("ck", 1, "float32"),
+    ("jc", 4, "float32"), ("CI", 144, "float32"), ("CB", 128, "float32"), ("C16", 16, "float32"),
+    ("Z1", 144, "bfloat16"), ("Z4", 144, "bfloat16"), ("Z8", 144, "bfloat16"), ("ZW", 144, "bfloat16"), ("Z0F", 144, "float32"),
+    ("BO", 128, "bfloat16"), ("BOW", 128, "bfloat16"), ("BON", 128, "bfloat16"), ("B0", 128, "float32"),
+    ("ID", 128, "bfloat16"), ("IZ", 128, "float32"), ("I0", 128, "float32"), ("ONF", 128, "float32"),
+    ("ON", 256, "bfloat16"), ("CSE", 128, "bfloat16"), ("CSO", 128, "bfloat16"),
+    ("AC", 128, "int32"), ("OC", 128, "int32"), ("ACF", 128, "float32"), ("OCF", 128, "float32"),
+    ("TI", 160, "float32"), ("TT", 160, "float32"), ("t0", 80, "float32"), ("t1", 80, "float32"), ("WW", 80, "float32"),
+    ("uI", 256, "int32"), ("uA", 256, "int32"), ("uwI", 64, "int32"), ("uwA", 64, "int32"), ("uwF", 64, "float32"),
+    ("pr", 64, "int32"), ("bs", 64, "int32"), ("OL", 1024, "uint16"), ("bt", 64, "int32"),
+    ("YR", 512, "float32"), ("yt", 256, "float32"), ("YH", 256, "float32"), ("YA", 1024, "float32"),
+    ("YV", 256, "float32"), ("YL", 256, "float32"),
+    ("SND", 256, "int32"), ("ARR", 256, "int32"),
+):
+    SCRATCH[_n] = ("sbuf", [128, _w], _d)
+PS = ("pK", "pE", "pO", "pD0", "pD1", "pC", "pW")
+for _n in PS:
+    SCRATCH[_n] = ("psum", [128, 512], "float32")
+SCRATCH["pT"] = ("psum", [128, 1024], "bfloat16")
+PSUM = PS + ("pT",)
+DMAS = {"lAC": 1, "lOC": 1, "lWT": 2, "lX": 1, "lXb": 1, "lR": 1, "gOW": 16, "gAA": 16, "gSX": 16,
+        "oR": 1, "oH": 1, "oA": 1, "oV": 1, "oL": 1}
+SEMAPHORES = ["V", "S", "P", "G", "snd"] + ["arr%d" % t for t in range(4)] + list(DMAS)
+
+
+def _meet(a, b):
+    if a[0] >= b[1] or b[0] >= a[1]:
+        return False
+    if a[2] == b[2]:
+        return a[2] == 1 or (a[0] - b[0]) % a[2] == 0
+    if a[2] == 1 or b[2] == 1:
+        if b[2] == 1:
+            a, b = b, a
+        first = b[0] + max(0, -((b[0] - a[0]) // b[2])) * b[2]
+        return first < min(a[1], b[1])
+    return True
+
+
+def _covers(a, b):
+    return a == b or (a[2] == 1 and a[0] <= b[0] and a[1] >= b[1])
+
+
+def rank_program(g, core, T, topo):
+    rank = T.rank_of(core)
+    if rank is None:
+        return
+    N = len(T.cores)
+    Q = {"V": g.vector, "S": g.scalar, "P": g.tensor, "G": g, "Y": g.sync}
+    count = {k: 0 for k in "VSPG"}
+    known = {k: {} for k in Q}
+    log = {}
+
+    def r(name, lo=0, hi=None, st=1):
+        return (name, lo, SCRATCH[name][1][1] if hi is None else hi, st)
+
+    def ap(x):
+        if len(x) == 2:
+            return ap(x[0]).indirect(ap(x[1]))
+        n, lo, hi, st = x
+        return T[n][:, lo:hi:st] if st > 1 else T[n][:, lo:hi]
+
+    def flat(xs):
+        out = []
+        for x in xs:
+            if isinstance(x, tuple):
+                if len(x) == 2:
+                    out += [x[0], x[1]]
+                else:
+                    out.append(x)
+        return out
+
+    def learn(eng, sem, val, clock):
+        kn = known[eng]
+        if kn.get(sem, 0) >= val:
+            return
+        Q[eng].wait_ge(T.sem[sem], val)
+        for s, x in clock.items():
+            if kn.get(s, 0) < x:
+                kn[s] = x
+        kn[sem] = max(kn.get(sem, 0), val)
+
+    def op(eng, fn, reads, writes, grp=None, inc=True):
+        reads, writes = flat(reads), flat(writes)
+        need = {}
+        for acc, wr in [(x, False) for x in reads] + [(x, True) for x in writes]:
+            bank = acc[0] in PSUM
+            for (sp, w2, eng2, sem, val, clock, grp2) in log.get(acc[0], ()):
+                if grp is not None and grp2 == grp:
+                    continue
+                if eng2 == eng and grp2 is None and grp is None:
+                    if (bank and eng == "P") or not (wr or w2) or not _meet(acc[1:], sp):
+                        continue
+                elif bank:
+                    pass
+                else:
+                    if not (wr or w2) or not _meet(acc[1:], sp):
+                        continue
+                if sem not in need or need[sem][0] < val:
+                    need[sem] = (val, clock)
+        for sem in sorted(need, key=lambda s: -len(need[s][1])):
+            learn(eng, sem, need[sem][0], need[sem][1])
+        ins = fn()
+        if grp is None:
+            count[eng] += 1
+            sem, val = eng, count[eng]
+            ins.then_inc(T.sem[sem], 1)
+        else:
+            sem, val = grp, 16 * DMAS[grp]
+            ins.then_inc(T.sem[sem], 16)
+        clock = dict(known[eng])
+        clock[sem] = val
+        for acc, wr in [(x, False) for x in reads] + [(x, True) for x in writes]:
+            old = log.setdefault(acc[0], [])
+            keep = []
+            for rec in old:
+                gone = False
+                if grp is None or rec[6] != grp:
+                    if wr and _covers(acc[1:], rec[0]):
+                        gone = True
+                    elif not wr and not rec[1] and rec[2] == eng and rec[6] is None and grp is None and _covers(acc[1:], rec[0]):
+                        gone = True
+                if not gone:
+                    keep.append(rec)
+            keep.append((acc[1:], wr, eng, sem, val, clock, grp))
+            log[acc[0]] = keep
+
+    def sc(x):
+        return ap(x) if isinstance(x, tuple) else x
+
+    def tt(o, a, b, f):
+        op("V", lambda: g.vector.tensor_tensor(out=ap(o), in0=ap(a), in1=ap(b), op=f), [a, b], [o])
+
+    def ts(o, a, s1, f, s2=None, f2=None):
+        if f2 is None:
+            op("V", lambda: g.vector.tensor_scalar(out=ap(o), in0=ap(a), scalar1=sc(s1), scalar2=None, op0=f), [a, s1], [o])
+        else:
+            op("V", lambda: g.vector.tensor_scalar(out=ap(o), in0=ap(a), scalar1=sc(s1), scalar2=sc(s2), op0=f, op1=f2), [a, s1, s2], [o])
+
+    def cp(o, a):
+        op("V", lambda: g.vector.tensor_copy(out=ap(o), in_=ap(a)), [a], [o])
+
+    def scatter(win, off, a):
+        op("V", lambda: g.vector.tensor_copy(out=ap((win, off)), in_=ap(a)), [a, off], [win])
+
+    def ms(o, c):
+        op("V", lambda: g.vector.memset(ap(o), c), [], [o])
+
+    def act(o, a, f=AF.Copy, bias=None, scale=None, acc=None):
+        kw = {}
+        if bias is not None:
+            kw["bias"] = sc(bias)
+        if scale is not None:
+            kw["scale"] = sc(scale)
+        if acc is not None:
+            kw["accum_out"] = ap(acc)
+        op("S", lambda: g.scalar.activation(out=ap(o), in_=ap(a), func=f, **kw), [a, bias, scale], [o] + ([acc] if acc else []))
+
+    def mm(o, l, x, start, stop):
+        op("P", lambda: g.tensor.matmul(out=ap(o), lhsT=ap(l), rhs=ap(x), start=start, stop=stop), [l, x], [o])
+
+    def dma(eng, out, in_, reads, writes, grp):
+        op(eng, lambda: Q[eng].dma_start(out=out, in_=in_), reads, writes, grp)
+
+    def iota(o, pattern, cm):
+        op("G", lambda: g.iota(ap(o), pattern, 0, cm, allow_small_or_imprecise_dtypes=True), [], [o])
+
+    def Z(name, k):
+        return r(name, 15 - k, 143 - k)
+
+    dma("Y", T["AC"][:], T["an"][:], [], [r("AC")], "lAC")
+    dma("S", T["X2"][:, 0:TW], T["xc"][:], [], [r("X2", 0, TW)], "lX")
+    dma("Y", T["OC"][:], T["rf"][0::16, :], [], [r("OC")], "lOC")
+    dma("Y", T["wI"][:], T["w"][:], [], [r("wI")], "lWT")
+    dma("Y", T["thI"][:], T["th"][:], [], [r("thI")], "lWT")
+    dma("S", T["X2"][:, TW:2 * TW], T["xc"][:], [], [r("X2", TW, 2 * TW)], "lXb")
+    dma("Y", T["R"][:, 0:TW], T["rf"][:], [], [r("R", 0, TW)], "lR")
+
+    iota(r("pI"), [[1, 1]], 1)
+    iota(r("CI"), [[1, 144]], 0)
+    iota(r("CB"), [[16, 8], [0, 16]], 0)
+    iota(r("C16"), [[16, 16]], 0)
+    ms(r("E"), -1.0)
+    cp(r("pF"), r("pI"))
+    ts(r("qI"), r("pI"), 112, OP.bitwise_and)
+    ts(r("rI"), r("pI"), 15, OP.bitwise_and)
+    ts(r("hI"), r("pI"), 4, OP.arith_shift_right, 1, OP.bitwise_and)
+    cp(r("q16"), r("qI"))
+    cp(r("rF"), r("rI"))
+    cp(r("m1"), r("hI"))
+    ts(r("c15"), r("qI"), 15.0, OP.add)
+    ts(r("m0"), r("m1"), 0.0, OP.is_equal)
+    ts(r("isz"), r("rF"), 0.0, OP.is_equal)
+    ts(r("inz"), r("rF"), 0.0, OP.not_equal)
+    ts(r("kI"), r("rI"), 613.0, OP.mult)
+    ts(r("kJ"), r("kI"), 2047, OP.bitwise_and)
+    cp(r("ck"), r("kJ"))
+    for c in range(4):
+        ts(r("jc", c, c + 1), r("rF"), 16.0 * c + 0.5, OP.add)
+    ts(r("vtw"), r("C16"), r("rF"), OP.add)
+    ts(r("vw"), r("vtw"), 8.0, OP.mult)
+    ts(r("AL", 16, 32), r("vtw"), float(TW), OP.add)
+    cp(r("ACF"), r("AC"))
+    for h in range(2):
+        cp(r("TI", 16 * h, 16 * h + 16), r("ACF", 0, 128, 8))
+    cp(r("OCF"), r("OC"))
+    for s in range(4):
+        for h in range(2):
+            cp(r("TI", 32 + 32 * s + 16 * h, 48 + 32 * s + 16 * h), r("OCF", s, 128, 8))
+    op("V", lambda: g.vector.transpose(out=ap(r("TT")), in_=ap(r("TI"))), [r("TI")], [r("TT")])
+    for n in range(5):
+        sl = (16 * n, 16 * n + 16)
+        ts(r("t0", *sl), r("TT", 32 * n, 32 * n + 16), r("m0"), OP.mult)
+        ts(r("t1", *sl), r("TT", 32 * n + 16, 32 * n + 32), r("m1"), OP.mult)
+    tt(r("WW"), r("t0"), r("t1"), OP.add)
+    cp(r("AL", 0, 16), r("WW", 0, 16))
+    for p in range(16):
+        dma("Y", T["OWB"][p::16, :], T["OCF"][:], [r("OCF")], [r("OWB")], "gOW")
+    for p in range(16):
+        dma("Y", T["AA"][p::16, 0:TW], T["ACF"][:], [r("ACF")], [r("AA", 0, TW)], "gAA")
+    cp(r("wF"), r("wI"))
+    CI = r("CI")
+    ts(r("ZW"), CI, r("c15"), OP.is_equal, r("wF"), OP.mult)
+    ts(r("BOW"), r("CB"), r("q16"), OP.is_equal, r("wF"), OP.mult)
+    ts(r("BON"), r("CB"), r("q16"), OP.is_equal, -4096.0, OP.mult)
+    ts(r("B0"), r("CB"), r("pF"), OP.is_equal)
+    C128 = r("CI", 0, 128)
+    ts(r("ID"), C128, r("pF"), OP.is_equal)
+    ts(r("IZ"), C128, r("pF"), OP.is_equal, r("inz"), OP.mult)
+    ts(r("I0"), C128, r("pF"), OP.is_equal, r("isz"), OP.mult)
+    ts(r("Z8"), CI, r("c15"), OP.is_equal, 8192.0, OP.mult)
+    ts(r("Z4"), CI, r("c15"), OP.is_equal, 4096.0, OP.mult)
+    ts(r("Z1"), CI, r("c15"), OP.is_equal)
+    ts(r("Z0F"), CI, r("c15"), OP.is_equal, r("isz"), OP.mult)
+    ts(r("BO"), r("CB"), r("q16"), OP.is_equal)
+    ms(r("ON"), 1.0)
+    ms(r("CSE"), -float(1 << 17))
+    ms(r("CSO"), -3.0 * (1 << 16))
+    ms(r("ONF"), 1.0)
+    ms(r("F", 256, 264), -4096)
+    ts(r("th4"), r("thI"), 4096.0, OP.mult, -float(1 << 24), OP.add)
+    op("G", lambda: g.affine_select(ap(r("E")), ap(r("E")), [[1, 2048]], OP.is_ge, 0.0, 0, -16), [r("E")], [r("E")])
+    op("G", lambda: g.affine_select(ap(r("E")), ap(r("E")), [[-1, 2048]], OP.is_ge, 0.0, 15, 16), [r("E")], [r("E")])
+    iota(r("IOT"), [[1, 2048]], 0)
+
+    def uw_p(s):
+        for p in range(16):
+            mm(r("pW", 64 + 16 * s, 80 + 16 * s), Z("ZW", p), r("X2", 8 * p + s, TW, 128), p == 0, p == 15)
+
+    def lists(lo, hi):
+        a, b = 16 * lo, 16 * hi
+        cp(r("uwI", a, b), r("pW", 64 + a, 64 + b))
+        ts(r("uwA", a, b), r("uwI", a, b), 4095, OP.bitwise_and)
+        ts(r("uwF", a, b), r("uwA", a, b), 32.0, OP.add)
+        tt(r("pr", a, b), r("uwF", a, b), r("WW", 16 + a, 16 + b), OP.mult)
+        ts(r("bs", a, b), r("pr", a, b), 5, OP.arith_shift_right, 2047, OP.bitwise_and)
+        for k in range(16):
+            ts(r("OL", 64 * k + a, 64 * k + b), r("bs", a, b), float(613 * k % TW), OP.add)
+
+    def utab_p(s):
+        mm(r("pC", 0, 256), r("BOW"), r("X2", s, TW, 8), True, True)
+
+    def utab_v(s):
+        cp(r("uI"), r("pC", 0, 256))
+        ts(r("uA"), r("uI"), 4095, OP.bitwise_and)
+        ts(r("U", 256 * s, 256 * s + 256), r("uA"), 32.0, OP.add)
+
+    def qs(s):
+        act(r("QS", 256 * s, 256 * s + 256), r("X2", s, TW, 8))
+
+    def own_v(s, ks):
+        for k in ks:
+            o = r("MX", 256 * k, 256 * k + 256)
+            tt(o, (r("X2"), r("OL", 64 * k + 16 * s, 64 * k + 16 * s + 16)), r("QS", 256 * s, 256 * s + 256), OP.max)
+
+    def own_p(s, ks):
+        o = r("pO", 0, 256)
+        for k in ks:
+            if k == 0:
+                mm(o, r("CSO"), r("ON"), True, False)
+                mm(o, r("BON"), r("QS", 256 * s, 256 * s + 256), False, False)
+            mm(o, Z("Z8", k), r("MX", 256 * k, 256 * k + 256), False, k == 15)
+
+    def own_w(s):
+        tt(r("wsx"), (r("SXS"), r("OL", 16 * s, 16 * s + 16)), r("OWB", s, TW, 8), OP.add)
+
+    def own_k(s):
+        tt(r("KN", 256 * s, 256 * s + 256), r("wsx"), r("pO", 0, 256), OP.add)
+
+    def stat(s):
+        act(r("OWN", 256 * s, 256 * s + 256), r("OWB", s, TW, 8))
+
+    uw_p(0)
+    utab_p(0)
+    lists(0, 1)
+    qs(0)
+    utab_v(0)
+    own_v(0, range(0, 4))
+    for c in range(4):
+        b = "pD%d" % (c % 2)
+        mm(r(b), r("BON"), r("X2", 512 * c, 512 * c + 512), True, True)
+        for h in range(2):
+            act(r("SXF", TW * h + 512 * c, TW * h + 512 * c + 512), r(b), AF.Identity, bias=float(4096 * 2048 + 2048))
+    for k in range(16):
+        d = 613 * k % TW
+        dma("Y", T["SXS"][k::16, :], T["SXF"][k::16, d:d + TW], [r("SXF")], [r("SXS")], "gSX")
+
+    NV = 128
+    pieces_v = [(0, 64), (64, 128)]
+    pieces_s = [(128, 192), (192, 256)]
+    for t in range(4):
+        if t == 0:
+            q, u, kn, ow = r("QS", 0, 256), r("U", 0, 256), r("KN", 0, 256), r("OWB", 0, TW, 8)
+        else:
+            n = 256 * (t + 1)
+            q, u, kn, ow = r("q"), r("u"), r("kn"), r("ow")
+            act(q, (r("QS", 0, n), r("VT16")))
+            act(u, (r("U", 0, n), r("VT16")))
+            act(ow, (r("OWN", 0, n), r("VT16")))
+        op("P", lambda: g.tensor.transpose(out=ap(r("pT", 0, 128)), in_=ap((q[0], q[1] + 128, q[1] + 256, 1)), identity=ap(r("ID"))),
+           [(q[0], q[1] + 128, q[1] + 256, 1), r("ID")], [r("pT", 0, 128)])
+        act(r("QT"), r("pT", 0, 128))
+        for k in range(16):
+            act(r("QX", k, 16 * NV, 16), (q[0], q[1], q[1] + NV, 1))
+        if t > 0:
+            act(r("aB"), (r("IOT"), r("AL", 0, 16)))
+            act(r("AB"), (r("AA", 0, TW + 256 * (t + 1)), r("AL")))
+            act(kn, (r("KN", 0, n), r("VT16")))
+            for p in range(16):
+                mm(r("pW", 0, 32), Z("Z0F", p), r("AB", p, 512, 16), p == 0, p == 15)
+            a, b = 64 * (t - 1), 64 * t
+            Q["V"].wait_ge(T.sem["arr%d" % (t - 1)], len(topo.engines(T.cores[(rank - t) % N], core)))
+            tt(r("bt"), r("ARR", a, b), r("R", 4 + t - 1, TW, 32), OP.max)
+            ts(r("R", 4 + t - 1, TW, 32), r("bt"), 2047, OP.bitwise_and)
+        cp(r("e"), (r("R", 0, TW), r("AL", 0, 16)))
+        tt(r("prod"), r("e"), u, OP.mult)
+        ts(r("pl"), r("prod"), 5, OP.arith_shift_right, 2047, OP.bitwise_and)
+        ts(r("pl16"), r("pl"), r("ck"), OP.add)
+        Ke = r("pK", 0, 256)
+        mm(Ke, r("CSE"), r("ON"), True, False)
+        mm(Ke, r("IZ"), r("e"), False, False)
+        mm(Ke, r("I0"), ow, False, False)
+        mm(r("pE", 0, 256), r("B0"), r("e"), True, True)
+
+        def sg(lo, hi):
+            act(r("XG", 16 * lo, 16 * hi), (r("X2"), r("pl16", lo, hi)))
+
+        def diff(lo, b):
+            mm(r(b), r("ID"), r("XG", 16 * lo, 16 * lo + 512), True, False)
+            mm(r(b), r("QT"), r("E", 16 * (lo - 128), 16 * (lo - 128) + 512), False, True)
+
+        def sums(lo, hi, last):
+            for k in range(16):
+                mm(r("pK", lo, hi), Z("Z4", k), r("AD", 16 * lo + k, 16 * hi, 16), False, last and k == 15)
+
+        for lo, hi in pieces_v:
+            tt(r("DD", 16 * lo, 16 * hi), (r("X2"), r("pl16", lo, hi)), r("QX", 16 * lo, 16 * hi), OP.subtract)
+        sg(128, 192)
+        act(r("AD", 0, 1024), r("DD", 0, 1024), AF.Abs)
+        sg(192, 256)
+        diff(128, "pD0")
+        diff(160, "pD1")
+        act(r("AD", 2048, 2560), r("pD0"), AF.Abs)
+        act(r("AD", 2560, 3072), r("pD1"), AF.Abs)
+        sums(0, 64, False)
+        diff(192, "pD0")
+        diff(224, "pD1")
+        act(r("AD", 1024, 2048), r("DD", 1024, 2048), AF.Abs)
+        sums(128, 192, False)
+        act(r("AD", 3072, 3584), r("pD0"), AF.Abs)
+        act(r("AD", 3584, 4096), r("pD1"), AF.Abs)
+        sums(64, 128, False)
+        sums(192, 256, True)
+        tt(r("eqs"), r("e"), r("pE", 0, 256), OP.is_equal)
+        if t == 0:
+            own_v(0, range(4, 16))
+            own_p(0, range(16))
+            own_w(0)
+            own_k(0)
+            for s in range(4):
+                stat(s)
+                act(r("AA", TW + 256 * s, TW + 256 * s + 256), r("AA", s + 1, TW, 8))
+                if s:
+                    qs(s)
+            act(r("aB"), (r("IOT"), r("AL", 0, 16)))
+            act(r("AB"), (r("AA", 0, TW + 256), r("AL")))
+            for p in range(16):
+                mm(r("pW", 0, 32), Z("Z0F", p), r("AB", p, 512, 16), p == 0, p == 15)
+            for s in range(1, 4):
+                uw_p(s)
+        tt(r("xk"), r("eqs"), kn, OP.mult)
+        cp(r("Aw"), r("pW", 0, 32))
+        tt(r("dA"), r("Aw", 16, 32), r("Aw", 0, 16), OP.subtract)
+        n1 = (0, 6, 6, 0)[t]
+        if 0 < t < 3:
+            own_v(t + 1, range(0, n1))
+        tt(r("m"), r("xk"), Ke, OP.min)
+        ts(r("hit"), r("m"), r("th4") if t == 0 else r("thb"), OP.is_lt)
+        mm(r("pC", 0, 256), r("BO"), r("hit"), True, True)
+        cw = r("pE", 256, 272)
+        for p in range(16):
+            mm(cw, Z("Z1", p), r("hit", p, 256, 16), p == 0, p == 15)
+        ts(r("F", 0, 256), r("m"), 2047, OP.bitwise_and)
+        ts(r("fitb"), r("pC", 0, 256), 7.5, OP.is_ge)
+        op("V", lambda: g.vector.tensor_tensor_scan(ap(r("cum")), ap(r("fitb")), ap(r("fitb")), 0.0, OP.add, OP.max),
+           [r("fitb")], [r("cum")])
+        for c in range(4):
+            act(r("junk"), r("cum"), AF.Sign, bias=r("jc", c, c + 1), scale=-1.0, acc=r("acc", c, c + 1))
+        ts(r("fit"), cw, 7.5, OP.is_ge)
+        ts(r("nf"), cw, 7.5, OP.is_lt, float(DUMP), OP.mult)
+        if t < 3:
+            ts(r("f256"), cw, 7.5, OP.is_ge, 256.0, OP.mult)
+        tt(r("tA"), r("fit"), r("dA"), OP.mult)
+        tt(r("vsw"), r("vw"), r("nf"), OP.add)
+        if t < 3:
+            tt(r("vtw"), r("vtw"), r("f256"), OP.add)
+        tt(r("aw"), r("tA"), r("Aw", 0, 16), OP.add)
+        tt(r("vw"), r("vw"), r("fit"), OP.add)
+        if t < 3:
+            cp(r("VT16"), r("vtw"))
+            ts(r("AL", 16, 32), r("vtw"), float(TW), OP.add)
+        cp(r("AL", 0, 16), r("aw"))
+        cp(r("VS16"), r("vsw"))
+        ts(r("inv16", 0, 4), r("acc"), 0.5, OP.mult, 128.0, OP.add)
+        snd = r("SND", 64 * t, 64 * t + 64)
+        ts(snd, (r("F"), r("inv16", 0, 4)), 4096.0, OP.add)
+        dst = T.cores[(rank + 1 + t % (N - 1)) % N]
+        rid, pid = topo.addr(dst, core)
+        last = log["SND"][-1]
+        learn("G", "V", last[4], last[5])
+        g.remote_dma(ap(r("ARR", 64 * t, 64 * t + 64)), ap(snd), T.sem["arr%d" % t], T.sem["snd"], pid, rid, topo.mask(core, dst))
+        scatter(r("R"), r("VS16"), r("F", 0, 256))
+        scatter(r("AA"), r("VS16"), r("aB"))
+        if t < 3:
+            mm(r("pE", 288, 304), r("ONF"), r("fit"), True, True)
+            if t == 0:
+                lists(1, 4)
+            s = t + 1
+            utab_p(s)
+            own_v(s, range(n1, 16))
+            own_p(s, range(16))
+            utab_v(s)
+            op("V", lambda: g.vector.tensor_reduce(ap(r("bsum")), ap(r("pE", 288, 304)), AxisListType.X, OP.add),
+               [r("pE", 288, 304)], [r("bsum")])
+            cp(r("bI", 0, 1), r("bsum"))
+            ts(r("bI", 1, 2), r("bI", 0, 1), 255, OP.bitwise_and)
+            ts(r("thb"), r("bI", 1, 2), 4096.0, OP.mult, r("th4"), OP.add)
+            own_w(s)
+            own_k(s)
+
+    cp(r("VT16"), r("vw"))
+    act(r("YL"), (r("IOT"), r("AL", 0, 16)))
+    dma("Y", T["ya"][:], T["YL"][0::16, :], [r("YL")], [], "oL")
+    act(r("YV"), (r("IOT"), r("VT16")))
+    dma("Y", T["yv"][:], T["YV"][0::16, :], [r("YV")], [], "oV")
+    for s in range(4):
+        act(r("YA", s, 1024, 4), r("AA", s, TW, 8))
+    dma("Y", T["yan"][:], T["YA"][0::16, :], [r("YA")], [], "oA")
+    for s in range(2):
+        yt = (r("yt"), r("junk"))[s]
+        ts(yt, r("R", 2 + s, TW, 8), 4096.0, OP.mult)
+        tt(r("YR", s, 512, 2), yt, r("R", s, TW, 8), OP.add)
+    dma("Y", T["yr"][:], T["YR"][:], [r("YR")], [], "oR")
+    for t in range(3):
+        cp(r("YH", t, 256, 4), r("R", 4 + t, TW, 32))
+    Q["V"].wait_ge(T.sem["arr3"], len(topo.engines(T.cores[(rank - 4) % N], core)))
+    tt(r("bt"), r("ARR", 192, 256), r("R", 7, TW, 32), OP.max)
+    ts(r("R", 7, TW, 32), r("bt"), 2047, OP.bitwise_and)
+    cp(r("YH", 3, 256, 4), r("R", 7, TW, 32))
+    dma("Y", T["yh"][:], T["YH"][:], [r("YH")], [], "oH")
+    for grp in DMAS:
+        g.wait_ge(T.sem[grp], 16 * DMAS[grp])
+    for e in "VSPG":
+        g.wait_ge(T.sem[e], count[e])
+    g.wait_ge(T.sem["snd"], sum(len(topo.engines(core, T.cores[(rank + 1 + t) % N])) for t in range(4)))

@@ -2,6 +2,15 @@ from concourse.mybir import AluOpType as OP, ActivationFunctionType as AF, AxisL
 
 TW = 2048
 DUMP = 3072
+KV = 12
+KA = 4
+N1 = (0, 4, 4, 0)
+W1 = 1
+W0 = 0
+NG = 10
+PLAN = (("Vq", 0, 64), ("Vq", 64, 128), ("Vg", 128, 160), ("Sg", 192, 256), ("Q", 0, 64), ("Sg", 160, 192),
+        ("D", 192, 0), ("D", 224, 1), ("A", 192, 0), ("A", 224, 1), ("M", 0, 64), ("D", 128, 0), ("K",), ("D", 160, 1),
+        ("Q", 64, 128), ("M", 192, 256), ("A", 128, 0), ("A", 160, 1), ("M", 64, 128), ("M", 128, 192))
 SCRATCH = {}
 for _n, _w, _d in (
     ("X2", 4096, "bfloat16"), ("R", 5120, "int32"), ("AA", 5120, "float32"), ("OWB", 2048, "float32"),
@@ -12,8 +21,8 @@ for _n, _w, _d in (
     ("ow", 256, "float32"), ("aB", 256, "float32"), ("AB", 512, "float32"), ("e", 256, "float32"),
     ("prod", 256, "int32"), ("pl", 256, "int32"), ("pl16", 256, "uint16"), ("eqs", 256, "float32"),
     ("xk", 256, "float32"), ("m", 256, "int32"), ("hit", 256, "bfloat16"), ("F", 264, "int32"),
-    ("fitb", 256, "float32"), ("cum", 256, "float32"), ("junk", 256, "float32"), ("acc", 4, "float32"),
-    ("inv16", 8, "uint16"), ("QT", 128, "bfloat16"), ("wsx", 256, "float32"),
+    ("fitb", 256, "float32"), ("cum", 256, "float32"), ("junk", 1024, "float32"), ("acc", 4, "float32"),
+    ("inv16", 8, "uint16"), ("QT", 256, "bfloat16"), ("wsx", 256, "float32"),
     ("fit", 16, "float32"), ("nf", 16, "float32"), ("f256", 16, "float32"), ("Aw", 32, "float32"), ("dA", 16, "float32"),
     ("tA", 16, "float32"), ("aw", 16, "float32"), ("vtw", 16, "float32"), ("vw", 16, "float32"), ("vsw", 16, "float32"),
     ("AL", 32, "uint16"), ("VT16", 16, "uint16"), ("VS16", 16, "uint16"),
@@ -21,17 +30,18 @@ for _n, _w, _d in (
     ("thI", 1, "int32"), ("wI", 1, "int32"), ("wF", 1, "float32"),
     ("pI", 1, "int32"), ("pF", 1, "float32"), ("qI", 1, "int32"), ("q16", 1, "float32"), ("c15", 1, "float32"),
     ("rI", 1, "int32"), ("rF", 1, "float32"), ("hI", 1, "int32"), ("m1", 1, "float32"), ("m0", 1, "float32"),
-    ("isz", 1, "float32"), ("inz", 1, "float32"), ("kI", 1, "int32"), ("kJ", 1, "int32"), ("ck", 1, "float32"),
+    ("kI", 2, "int32"), ("ck", 1, "float32"),
     ("jc", 4, "float32"), ("CI", 144, "float32"), ("CB", 128, "float32"), ("C16", 16, "float32"),
     ("Z1", 144, "bfloat16"), ("Z4", 144, "bfloat16"), ("Z8", 144, "bfloat16"), ("ZW", 144, "bfloat16"), ("Z0F", 144, "float32"),
     ("BO", 128, "bfloat16"), ("BOW", 128, "bfloat16"), ("BON", 128, "bfloat16"), ("B0", 128, "float32"),
-    ("ID", 128, "bfloat16"), ("IZ", 128, "float32"), ("I0", 128, "float32"), ("ONF", 128, "float32"),
+    ("ID", 128, "bfloat16"), ("NI", 128, "bfloat16"), ("IZ", 128, "float32"), ("I0", 128, "float32"),
+    ("IDF", 128, "float32"), ("ONF", 144, "float32"),
     ("ON", 256, "bfloat16"), ("CSE", 128, "bfloat16"), ("CSO", 128, "bfloat16"),
     ("AC", 128, "int32"), ("OC", 128, "int32"), ("ACF", 128, "float32"), ("OCF", 128, "float32"),
     ("TI", 160, "float32"), ("TT", 160, "float32"), ("t0", 80, "float32"), ("t1", 80, "float32"), ("WW", 80, "float32"),
     ("uI", 256, "int32"), ("uA", 256, "int32"), ("uwI", 64, "int32"), ("uwA", 64, "int32"), ("uwF", 64, "float32"),
     ("pr", 64, "int32"), ("bs", 64, "int32"), ("OL", 1024, "uint16"), ("bt", 64, "int32"),
-    ("YR", 512, "float32"), ("yt", 256, "float32"), ("YH", 256, "float32"), ("YA", 1024, "float32"),
+    ("YR", 512, "float32"), ("YH", 256, "float32"), ("YA", 1024, "float32"),
     ("YV", 256, "float32"), ("YL", 256, "float32"),
     ("SND", 256, "int32"), ("ARR", 256, "int32"),
 ):
@@ -41,7 +51,7 @@ for _n in PS:
     SCRATCH[_n] = ("psum", [128, 512], "float32")
 SCRATCH["pT"] = ("psum", [128, 1024], "bfloat16")
 PSUM = PS + ("pT",)
-DMAS = {"lAC": 1, "lOC": 1, "lWT": 2, "lX": 1, "lXb": 1, "lR": 1, "gOW": 16, "gAA": 16, "gSX": 16,
+DMAS = {"lAC": 1, "lOC": 1, "lWT": 2, "lX": 1, "lXb": 1, "lR": 1, "gOW": 16, "gAA": 16, "gSF": 1, "gSX": 16,
         "oR": 1, "oH": 1, "oA": 1, "oV": 1, "oL": 1}
 SEMAPHORES = ["V", "S", "P", "G", "snd"] + ["arr%d" % t for t in range(4)] + list(DMAS)
 
@@ -102,7 +112,7 @@ def rank_program(g, core, T, topo):
                 kn[s] = x
         kn[sem] = max(kn.get(sem, 0), val)
 
-    def op(eng, fn, reads, writes, grp=None, inc=True):
+    def op(eng, fn, reads, writes, grp=None):
         reads, writes = flat(reads), flat(writes)
         need = {}
         for acc, wr in [(x, False) for x in reads] + [(x, True) for x in writes]:
@@ -165,9 +175,6 @@ def rank_program(g, core, T, topo):
     def scatter(win, off, a):
         op("V", lambda: g.vector.tensor_copy(out=ap((win, off)), in_=ap(a)), [a, off], [win])
 
-    def ms(o, c):
-        op("V", lambda: g.vector.memset(ap(o), c), [], [o])
-
     def act(o, a, f=AF.Copy, bias=None, scale=None, acc=None):
         kw = {}
         if bias is not None:
@@ -184,8 +191,11 @@ def rank_program(g, core, T, topo):
     def dma(eng, out, in_, reads, writes, grp):
         op(eng, lambda: Q[eng].dma_start(out=out, in_=in_), reads, writes, grp)
 
-    def iota(o, pattern, cm):
-        op("G", lambda: g.iota(ap(o), pattern, 0, cm, allow_small_or_imprecise_dtypes=True), [], [o])
+    def iota(o, pattern, cm, base=0):
+        op("G", lambda: g.iota(ap(o), pattern, base, cm, allow_small_or_imprecise_dtypes=True), [], [o])
+
+    def sel(o, a, pattern, cmp, base, cm):
+        op("G", lambda: g.affine_select(ap(o), ap(a), pattern, cmp, 0.0, base, cm), [a], [o])
 
     def Z(name, k):
         return r(name, 15 - k, 143 - k)
@@ -199,10 +209,11 @@ def rank_program(g, core, T, topo):
     dma("Y", T["R"][:, 0:TW], T["rf"][:], [], [r("R", 0, TW)], "lR")
 
     iota(r("pI"), [[1, 1]], 1)
-    iota(r("CI"), [[1, 144]], 0)
     iota(r("CB"), [[16, 8], [0, 16]], 0)
+    iota(r("CI"), [[1, 144]], 0)
     iota(r("C16"), [[16, 16]], 0)
-    ms(r("E"), -1.0)
+    for name, c in (("ON", 1), ("CSO", -3 * (1 << 16)), ("CSE", -(1 << 17)), ("ONF", 1)):
+        iota(r(name), [[0, SCRATCH[name][1][1]]], 0, c)
     cp(r("pF"), r("pI"))
     ts(r("qI"), r("pI"), 112, OP.bitwise_and)
     ts(r("rI"), r("pI"), 15, OP.bitwise_and)
@@ -211,58 +222,55 @@ def rank_program(g, core, T, topo):
     cp(r("rF"), r("rI"))
     cp(r("m1"), r("hI"))
     ts(r("c15"), r("qI"), 15.0, OP.add)
+    CI, C128 = r("CI"), r("CI", 0, 128)
+    ts(r("BON"), r("CB"), r("q16"), OP.is_equal, -4096.0, OP.mult)
+    sel(r("BON"), r("BON"), [[0, 8], [-1, 16]], OP.is_ge, KV - 1, 0)
+    O8 = r("ONF", 0, 128)
+    sel(r("IZ"), O8, [[-1, 128]], OP.is_equal, 0, 1)
+    sel(r("IZ"), r("IZ"), [[0, 8], [1, 16]], OP.not_equal, 0, 0)
+    sel(r("B0"), O8, [[-16, 8], [0, 16]], OP.is_equal, 0, 1)
+    sel(r("I0"), O8, [[-16, 8], [-1000, 16]], OP.is_equal, 0, 1)
+    sel(r("IDF"), O8, [[-1, 128]], OP.is_equal, 0, 1)
     ts(r("m0"), r("m1"), 0.0, OP.is_equal)
-    ts(r("isz"), r("rF"), 0.0, OP.is_equal)
-    ts(r("inz"), r("rF"), 0.0, OP.not_equal)
-    ts(r("kI"), r("rI"), 613.0, OP.mult)
-    ts(r("kJ"), r("kI"), 2047, OP.bitwise_and)
-    cp(r("ck"), r("kJ"))
+    ts(r("kI", 0, 1), r("rI"), 613.0, OP.mult)
+    ts(r("vtw"), r("C16"), r("rF"), OP.add)
+    ts(r("kI", 1, 2), r("kI", 0, 1), 2047, OP.bitwise_and)
     for c in range(4):
         ts(r("jc", c, c + 1), r("rF"), 16.0 * c + 0.5, OP.add)
-    ts(r("vtw"), r("C16"), r("rF"), OP.add)
     ts(r("vw"), r("vtw"), 8.0, OP.mult)
+    cp(r("ck"), r("kI", 1, 2))
     ts(r("AL", 16, 32), r("vtw"), float(TW), OP.add)
-    cp(r("ACF"), r("AC"))
-    for h in range(2):
-        cp(r("TI", 16 * h, 16 * h + 16), r("ACF", 0, 128, 8))
     cp(r("OCF"), r("OC"))
+    cp(r("ACF"), r("AC"))
+    cp(r("wF"), r("wI"))
     for s in range(4):
         for h in range(2):
-            cp(r("TI", 32 + 32 * s + 16 * h, 48 + 32 * s + 16 * h), r("OCF", s, 128, 8))
+            act(r("TI", 32 + 32 * s + 16 * h, 48 + 32 * s + 16 * h), r("OCF", s, 128, 8))
+    ts(r("ZW"), CI, r("c15"), OP.is_equal, r("wF"), OP.mult)
+    ts(r("BOW"), r("CB"), r("q16"), OP.is_equal, r("wF"), OP.mult)
+    for h in range(2):
+        act(r("TI", 16 * h, 16 * h + 16), r("ACF", 0, 128, 8))
+    ts(r("ID"), C128, r("pF"), OP.is_equal)
     op("V", lambda: g.vector.transpose(out=ap(r("TT")), in_=ap(r("TI"))), [r("TI")], [r("TT")])
+    ts(r("NI"), C128, r("pF"), OP.is_equal, -1.0, OP.mult)
     for n in range(5):
         sl = (16 * n, 16 * n + 16)
-        ts(r("t0", *sl), r("TT", 32 * n, 32 * n + 16), r("m0"), OP.mult)
+        act(r("t0", *sl), r("TT", 32 * n, 32 * n + 16), AF.Copy, scale=r("m0"))
         ts(r("t1", *sl), r("TT", 32 * n + 16, 32 * n + 32), r("m1"), OP.mult)
     tt(r("WW"), r("t0"), r("t1"), OP.add)
+    ts(r("Z4"), CI, r("c15"), OP.is_equal, 4096.0, OP.mult)
     cp(r("AL", 0, 16), r("WW", 0, 16))
     for p in range(16):
         dma("Y", T["OWB"][p::16, :], T["OCF"][:], [r("OCF")], [r("OWB")], "gOW")
     for p in range(16):
         dma("Y", T["AA"][p::16, 0:TW], T["ACF"][:], [r("ACF")], [r("AA", 0, TW)], "gAA")
-    cp(r("wF"), r("wI"))
-    CI = r("CI")
-    ts(r("ZW"), CI, r("c15"), OP.is_equal, r("wF"), OP.mult)
-    ts(r("BOW"), r("CB"), r("q16"), OP.is_equal, r("wF"), OP.mult)
-    ts(r("BON"), r("CB"), r("q16"), OP.is_equal, -4096.0, OP.mult)
-    ts(r("B0"), r("CB"), r("pF"), OP.is_equal)
-    C128 = r("CI", 0, 128)
-    ts(r("ID"), C128, r("pF"), OP.is_equal)
-    ts(r("IZ"), C128, r("pF"), OP.is_equal, r("inz"), OP.mult)
-    ts(r("I0"), C128, r("pF"), OP.is_equal, r("isz"), OP.mult)
-    ts(r("Z8"), CI, r("c15"), OP.is_equal, 8192.0, OP.mult)
-    ts(r("Z4"), CI, r("c15"), OP.is_equal, 4096.0, OP.mult)
-    ts(r("Z1"), CI, r("c15"), OP.is_equal)
-    ts(r("Z0F"), CI, r("c15"), OP.is_equal, r("isz"), OP.mult)
-    ts(r("BO"), r("CB"), r("q16"), OP.is_equal)
-    ms(r("ON"), 1.0)
-    ms(r("CSE"), -float(1 << 17))
-    ms(r("CSO"), -3.0 * (1 << 16))
-    ms(r("ONF"), 1.0)
-    ms(r("F", 256, 264), -4096)
-    ts(r("th4"), r("thI"), 4096.0, OP.mult, -float(1 << 24), OP.add)
-    op("G", lambda: g.affine_select(ap(r("E")), ap(r("E")), [[1, 2048]], OP.is_ge, 0.0, 0, -16), [r("E")], [r("E")])
-    op("G", lambda: g.affine_select(ap(r("E")), ap(r("E")), [[-1, 2048]], OP.is_ge, 0.0, 15, 16), [r("E")], [r("E")])
+    for k in range(16):
+        sel(r("E", k, 2048, 16), r("NI"), [[0, 128]], OP.is_equal, 0, 0)
+    sel(r("Z0F"), r("ONF"), [[16, 9], [1000, 16]], OP.is_equal, -15000, -1)
+    for o in ("BO", "Z1"):
+        w, x = (128, 0) if o == "BO" else (144, 1000)
+        sel(r(o), r("ON", 0, w), [[-16, w // 16], [x, 16]], OP.is_ge, -15 * x, 1)
+        sel(r(o), r(o), [[16, w // 16], [0, 16]], OP.is_ge, 15, -1)
     iota(r("IOT"), [[1, 2048]], 0)
 
     def uw_p(s):
@@ -276,7 +284,7 @@ def rank_program(g, core, T, topo):
         ts(r("uwF", a, b), r("uwA", a, b), 32.0, OP.add)
         tt(r("pr", a, b), r("uwF", a, b), r("WW", 16 + a, 16 + b), OP.mult)
         ts(r("bs", a, b), r("pr", a, b), 5, OP.arith_shift_right, 2047, OP.bitwise_and)
-        for k in range(16):
+        for k in list(range(KV, 16)) + list(range(KV)):
             ts(r("OL", 64 * k + a, 64 * k + b), r("bs", a, b), float(613 * k % TW), OP.add)
 
     def utab_p(s):
@@ -292,16 +300,34 @@ def rank_program(g, core, T, topo):
 
     def own_v(s, ks):
         for k in ks:
-            o = r("MX", 256 * k, 256 * k + 256)
-            tt(o, (r("X2"), r("OL", 64 * k + 16 * s, 64 * k + 16 * s + 16)), r("QS", 256 * s, 256 * s + 256), OP.max)
+            tt(r("MX", 256 * k, 256 * k + 256), (r("X2"), r("OL", 64 * k + 16 * s, 64 * k + 16 * s + 16)),
+               r("QS", 256 * s, 256 * s + 256), OP.max)
 
-    def own_p(s, ks):
-        o = r("pO", 0, 256)
+    SA, SB = list(range(KV, KV + KA)), list(range(KV + KA, 16))
+
+    def own_sg(s, ks):
         for k in ks:
-            if k == 0:
-                mm(o, r("CSO"), r("ON"), True, False)
-                mm(o, r("BON"), r("QS", 256 * s, 256 * s + 256), False, False)
-            mm(o, Z("Z8", k), r("MX", 256 * k, 256 * k + 256), False, k == 15)
+            act(r("XG", 256 * (k - KV), 256 * (k - KV) + 256), (r("X2"), r("OL", 64 * k + 16 * s, 64 * k + 16 * s + 16)))
+
+    def own_sd(s, ks):
+        for k in ks[::2]:
+            b = "pD%d" % (k // 2 % 2)
+            mm(r(b), r("ID"), r("XG", 256 * (k - KV), 256 * (k - KV) + 512), True, False)
+            for h in range(2):
+                mm(r(b, 256 * h, 256 * h + 256), r("NI"), r("QS", 256 * s, 256 * s + 256), False, h == 1)
+
+    def own_sa(ks):
+        for k in ks[::2]:
+            act(r("MX", 256 * k, 256 * k + 512), r("pD%d" % (k // 2 % 2)), AF.Abs)
+
+    def own_p(s, ks, first=False, last=False):
+        o = r("pO", 0, 256)
+        if first:
+            mm(o, r("CSO"), r("ON"), True, False)
+            mm(o, r("BON"), r("QS", 256 * s, 256 * s + 256), False, False)
+        ks = list(ks)
+        for k in ks:
+            mm(o, Z("Z8" if k < KV else "Z4", k), r("MX", 256 * k, 256 * k + 256), False, last and k == ks[-1])
 
     def own_w(s):
         tt(r("wsx"), (r("SXS"), r("OL", 16 * s, 16 * s + 16)), r("OWB", s, TW, 8), OP.add)
@@ -309,47 +335,53 @@ def rank_program(g, core, T, topo):
     def own_k(s):
         tt(r("KN", 256 * s, 256 * s + 256), r("wsx"), r("pO", 0, 256), OP.add)
 
-    def stat(s):
-        act(r("OWN", 256 * s, 256 * s + 256), r("OWB", s, TW, 8))
+    def wrap():
+        for p in range(16):
+            mm(r("pW", 0, 32), Z("Z0F", p), r("AB", p, 512, 16), p == 0, p == 15)
+
+    HALVES = sorted({x[1] // 128 for x in PLAN if x[0] == "D"})
+    NQ = sum(x[2] - x[1] for x in PLAN if x[0] == "Vq")
+
+    def turn(q):
+        for h in HALVES:
+            src = (q[0], q[1] + 128 * h, q[1] + 128 * h + 128, 1)
+            op("P", lambda: g.tensor.transpose(out=ap(r("pT", 128 * h, 128 * h + 128)), in_=ap(src), identity=ap(r("ID"))),
+               [src, r("ID")], [r("pT", 128 * h, 128 * h + 128)])
+        a, b = 128 * HALVES[0], 128 * HALVES[-1] + 128
+        act(r("QT", a, b), r("pT", a, b))
+
+    def spread(q, ng):
+        src = (q[0], q[1], q[1] + NQ, 1)
+        for k in range(16):
+            if k < 16 - ng:
+                act(r("QX", k, 16 * NQ, 16), src)
+            else:
+                sel(r("QX", k, 16 * NQ, 16), src, [[0, NQ]], OP.is_equal, 0, 0)
 
     uw_p(0)
     utab_p(0)
-    lists(0, 1)
     qs(0)
+    lists(0, 1)
     utab_v(0)
-    own_v(0, range(0, 4))
+    turn(r("QS", 0, 256))
+    spread(r("QS", 0, 256), 0)
     for c in range(4):
         b = "pD%d" % (c % 2)
         mm(r(b), r("BON"), r("X2", 512 * c, 512 * c + 512), True, True)
-        for h in range(2):
-            act(r("SXF", TW * h + 512 * c, TW * h + 512 * c + 512), r(b), AF.Identity, bias=float(4096 * 2048 + 2048))
+        act(r("SXF", 512 * c, 512 * c + 512), r(b), AF.Identity, bias=float(4096 * 2048 + 2048))
+    dma("Y", T["SXF"][:, TW:2 * TW], T["SXF"][:, 0:TW], [r("SXF", 0, TW)], [r("SXF", TW, 2 * TW)], "gSF")
     for k in range(16):
         d = 613 * k % TW
         dma("Y", T["SXS"][k::16, :], T["SXF"][k::16, d:d + TW], [r("SXF")], [r("SXS")], "gSX")
+    own_v(0, range(0, W0))
+    for s in range(1, 4):
+        uw_p(s)
 
-    NV = 128
-    pieces_v = [(0, 64), (64, 128)]
-    pieces_s = [(128, 192), (192, 256)]
     for t in range(4):
         if t == 0:
-            q, u, kn, ow = r("QS", 0, 256), r("U", 0, 256), r("KN", 0, 256), r("OWB", 0, TW, 8)
+            u, kn, ow = r("U", 0, 256), r("KN", 0, 256), r("OWB", 0, TW, 8)
         else:
-            n = 256 * (t + 1)
-            q, u, kn, ow = r("q"), r("u"), r("kn"), r("ow")
-            act(q, (r("QS", 0, n), r("VT16")))
-            act(u, (r("U", 0, n), r("VT16")))
-            act(ow, (r("OWN", 0, n), r("VT16")))
-        op("P", lambda: g.tensor.transpose(out=ap(r("pT", 0, 128)), in_=ap((q[0], q[1] + 128, q[1] + 256, 1)), identity=ap(r("ID"))),
-           [(q[0], q[1] + 128, q[1] + 256, 1), r("ID")], [r("pT", 0, 128)])
-        act(r("QT"), r("pT", 0, 128))
-        for k in range(16):
-            act(r("QX", k, 16 * NV, 16), (q[0], q[1], q[1] + NV, 1))
-        if t > 0:
-            act(r("aB"), (r("IOT"), r("AL", 0, 16)))
-            act(r("AB"), (r("AA", 0, TW + 256 * (t + 1)), r("AL")))
-            act(kn, (r("KN", 0, n), r("VT16")))
-            for p in range(16):
-                mm(r("pW", 0, 32), Z("Z0F", p), r("AB", p, 512, 16), p == 0, p == 15)
+            u, kn, ow = r("pE", 0, 256), r("pW", 128, 384), r("ow")
             a, b = 64 * (t - 1), 64 * t
             Q["V"].wait_ge(T.sem["arr%d" % (t - 1)], len(topo.engines(T.cores[(rank - t) % N], core)))
             tt(r("bt"), r("ARR", a, b), r("R", 4 + t - 1, TW, 32), OP.max)
@@ -358,64 +390,73 @@ def rank_program(g, core, T, topo):
         tt(r("prod"), r("e"), u, OP.mult)
         ts(r("pl"), r("prod"), 5, OP.arith_shift_right, 2047, OP.bitwise_and)
         ts(r("pl16"), r("pl"), r("ck"), OP.add)
+        if t < 3:
+            utab_p(t + 1)
         Ke = r("pK", 0, 256)
         mm(Ke, r("CSE"), r("ON"), True, False)
-        mm(Ke, r("IZ"), r("e"), False, False)
         mm(Ke, r("I0"), ow, False, False)
+        mm(Ke, r("IZ"), r("e"), False, False)
         mm(r("pE", 0, 256), r("B0"), r("e"), True, True)
-
-        def sg(lo, hi):
-            act(r("XG", 16 * lo, 16 * hi), (r("X2"), r("pl16", lo, hi)))
-
-        def diff(lo, b):
-            mm(r(b), r("ID"), r("XG", 16 * lo, 16 * lo + 512), True, False)
-            mm(r(b), r("QT"), r("E", 16 * (lo - 128), 16 * (lo - 128) + 512), False, True)
-
-        def sums(lo, hi, last):
-            for k in range(16):
-                mm(r("pK", lo, hi), Z("Z4", k), r("AD", 16 * lo + k, 16 * hi, 16), False, last and k == 15)
-
-        for lo, hi in pieces_v:
-            tt(r("DD", 16 * lo, 16 * hi), (r("X2"), r("pl16", lo, hi)), r("QX", 16 * lo, 16 * hi), OP.subtract)
-        sg(128, 192)
-        act(r("AD", 0, 1024), r("DD", 0, 1024), AF.Abs)
-        sg(192, 256)
-        diff(128, "pD0")
-        diff(160, "pD1")
-        act(r("AD", 2048, 2560), r("pD0"), AF.Abs)
-        act(r("AD", 2560, 3072), r("pD1"), AF.Abs)
-        sums(0, 64, False)
-        diff(192, "pD0")
-        diff(224, "pD1")
-        act(r("AD", 1024, 2048), r("DD", 1024, 2048), AF.Abs)
-        sums(128, 192, False)
-        act(r("AD", 3072, 3584), r("pD0"), AF.Abs)
-        act(r("AD", 3584, 4096), r("pD1"), AF.Abs)
-        sums(64, 128, False)
-        sums(192, 256, True)
+        lastm = [x for x in PLAN if x[0] == "M"][-1]
+        for x in PLAN:
+            if x[0] == "Vq":
+                lo, hi = x[1:]
+                tt(r("DD", 16 * lo, 16 * hi), (r("X2"), r("pl16", lo, hi)), r("QX", 16 * lo, 16 * hi), OP.subtract)
+            elif x[0] == "Vg":
+                lo, hi = x[1:]
+                cp(r("XG", 16 * lo, 16 * hi), (r("X2"), r("pl16", lo, hi)))
+            elif x[0] == "Sg":
+                lo, hi = x[1:]
+                act(r("XG", 16 * lo, 16 * hi), (r("X2"), r("pl16", lo, hi)))
+            elif x[0] == "Q":
+                lo, hi = x[1:]
+                act(r("AD", 16 * lo, 16 * hi), r("DD", 16 * lo, 16 * hi), AF.Abs)
+            elif x[0] == "D":
+                lo, b, h = x[1], "pD%d" % x[2], x[1] // 128
+                mm(r(b), r("ID"), r("XG", 16 * lo, 16 * lo + 512), True, False)
+                mm(r(b), r("QT", 128 * h, 128 * h + 128), r("E", 16 * (lo - 128 * h), 16 * (lo - 128 * h) + 512), False, True)
+            elif x[0] == "A":
+                act(r("AD", 16 * x[1], 16 * x[1] + 512), r("pD%d" % x[2]), AF.Abs)
+            elif x[0] == "M":
+                lo, hi = x[1:]
+                for k in range(16):
+                    mm(r("pK", lo, hi), Z("Z4", k), r("AD", 16 * lo + k, 16 * hi, 16), False, x is lastm and k == 15)
+            elif t > 0:
+                own_w(t)
+                own_k(t)
+                act(r("kn"), (r("KN", 0, 256 * (t + 1)), r("VT16")))
+                mm(kn, r("IDF"), r("kn"), True, True)
+        if t == 0:
+            ts(r("Z8"), CI, r("c15"), OP.is_equal, 8192.0, OP.mult)
+            op("V", lambda: g.vector.memset(ap(r("F", 256, 264)), -4096), [], [r("F", 256, 264)])
+            ts(r("th4"), r("thI"), 4096.0, OP.mult, -float(1 << 24), OP.add)
+            own_v(0, range(W0, KV))
+            act(r("AA", TW, TW + 256), r("AA", 1, TW, 8))
+            act(r("AB"), (r("AA", 0, TW + 256), r("AL")))
+            wrap()
+            own_sg(0, SA + SB)
+            own_p(0, range(KV), True)
+            own_sd(0, SA + SB)
+            own_sa(SA + SB)
+            own_p(0, SA + SB, False, True)
+        if t < 3:
+            utab_v(t + 1)
         tt(r("eqs"), r("e"), r("pE", 0, 256), OP.is_equal)
         if t == 0:
-            own_v(0, range(4, 16))
-            own_p(0, range(16))
             own_w(0)
+            lists(1, 4)
             own_k(0)
-            for s in range(4):
-                stat(s)
-                act(r("AA", TW + 256 * s, TW + 256 * s + 256), r("AA", s + 1, TW, 8))
-                if s:
-                    qs(s)
-            act(r("aB"), (r("IOT"), r("AL", 0, 16)))
-            act(r("AB"), (r("AA", 0, TW + 256), r("AL")))
-            for p in range(16):
-                mm(r("pW", 0, 32), Z("Z0F", p), r("AB", p, 512, 16), p == 0, p == 15)
             for s in range(1, 4):
-                uw_p(s)
+                qs(s)
+                act(r("AA", TW + 256 * s, TW + 256 * s + 256), r("AA", s + 1, TW, 8))
+            act(r("aB"), (r("IOT"), r("AL", 0, 16)))
         tt(r("xk"), r("eqs"), kn, OP.mult)
         cp(r("Aw"), r("pW", 0, 32))
         tt(r("dA"), r("Aw", 16, 32), r("Aw", 0, 16), OP.subtract)
-        n1 = (0, 6, 6, 0)[t]
-        if 0 < t < 3:
+        n1 = N1[t]
+        if t < 3:
             own_v(t + 1, range(0, n1))
+            own_sg(t + 1, SA)
         tt(r("m"), r("xk"), Ke, OP.min)
         ts(r("hit"), r("m"), r("th4") if t == 0 else r("thb"), OP.is_lt)
         mm(r("pC", 0, 256), r("BO"), r("hit"), True, True)
@@ -427,7 +468,7 @@ def rank_program(g, core, T, topo):
         op("V", lambda: g.vector.tensor_tensor_scan(ap(r("cum")), ap(r("fitb")), ap(r("fitb")), 0.0, OP.add, OP.max),
            [r("fitb")], [r("cum")])
         for c in range(4):
-            act(r("junk"), r("cum"), AF.Sign, bias=r("jc", c, c + 1), scale=-1.0, acc=r("acc", c, c + 1))
+            act(r("junk", 256 * c, 256 * c + 256), r("cum"), AF.Sign, bias=r("jc", c, c + 1), scale=-1.0, acc=r("acc", c, c + 1))
         ts(r("fit"), cw, 7.5, OP.is_ge)
         ts(r("nf"), cw, 7.5, OP.is_lt, float(DUMP), OP.mult)
         if t < 3:
@@ -443,6 +484,12 @@ def rank_program(g, core, T, topo):
             ts(r("AL", 16, 32), r("vtw"), float(TW), OP.add)
         cp(r("AL", 0, 16), r("aw"))
         cp(r("VS16"), r("vsw"))
+        if t < 3:
+            own_sd(t + 1, SA)
+            own_sa(SA)
+            own_v(t + 1, range(n1, n1 + W1))
+        else:
+            scatter(r("AA"), r("VS16"), r("aB"))
         ts(r("inv16", 0, 4), r("acc"), 0.5, OP.mult, 128.0, OP.add)
         snd = r("SND", 64 * t, 64 * t + 64)
         ts(snd, (r("F"), r("inv16", 0, 4)), 4096.0, OP.add)
@@ -451,38 +498,51 @@ def rank_program(g, core, T, topo):
         last = log["SND"][-1]
         learn("G", "V", last[4], last[5])
         g.remote_dma(ap(r("ARR", 64 * t, 64 * t + 64)), ap(snd), T.sem["arr%d" % t], T.sem["snd"], pid, rid, topo.mask(core, dst))
-        scatter(r("R"), r("VS16"), r("F", 0, 256))
-        scatter(r("AA"), r("VS16"), r("aB"))
         if t < 3:
-            mm(r("pE", 288, 304), r("ONF"), r("fit"), True, True)
-            if t == 0:
-                lists(1, 4)
-            s = t + 1
-            utab_p(s)
-            own_v(s, range(n1, 16))
-            own_p(s, range(16))
-            utab_v(s)
+            mm(r("pE", 288, 304), r("ONF", 0, 128), r("fit"), True, True)
+            scatter(r("AA"), r("VS16"), r("aB"))
             op("V", lambda: g.vector.tensor_reduce(ap(r("bsum")), ap(r("pE", 288, 304)), AxisListType.X, OP.add),
                [r("pE", 288, 304)], [r("bsum")])
+        scatter(r("R"), r("VS16"), r("F", 0, 256))
+        if t < 3:
+            s, n = t + 1, 256 * (t + 2)
+            act(r("q"), (r("QS", 0, n), r("VT16")))
+            turn(r("q"))
+            act(r("u"), (r("U", 0, n), r("VT16")))
+            mm(r("pE", 0, 256), r("IDF"), r("u"), True, True)
+            if t == 0:
+                for c in range(4):
+                    act(r("OWN", 256 * c, 256 * c + 256), r("OWB", c, TW, 8))
+            act(r("AB"), (r("AA", 0, TW + n), r("AL")))
+            own_p(s, list(range(0, n1 + W1)) + SA, True)
+            spread(r("q"), NG)
+            own_sg(s, SB)
+            own_sd(s, SB)
+            wrap()
+            act(r("ow"), (r("OWN", 0, n), r("VT16")))
+            own_sa(SB)
+            act(r("aB"), (r("IOT"), r("AL", 0, 16)))
+            own_v(s, range(n1 + W1, n1 + W1 + 1))
             cp(r("bI", 0, 1), r("bsum"))
+            own_v(s, range(n1 + W1 + 1, n1 + W1 + 2))
             ts(r("bI", 1, 2), r("bI", 0, 1), 255, OP.bitwise_and)
+            own_v(s, range(n1 + W1 + 2, KV))
             ts(r("thb"), r("bI", 1, 2), 4096.0, OP.mult, r("th4"), OP.add)
-            own_w(s)
-            own_k(s)
+            own_p(s, SB + list(range(n1 + W1, KV)), False, True)
 
     cp(r("VT16"), r("vw"))
-    act(r("YL"), (r("IOT"), r("AL", 0, 16)))
-    dma("Y", T["ya"][:], T["YL"][0::16, :], [r("YL")], [], "oL")
-    act(r("YV"), (r("IOT"), r("VT16")))
-    dma("Y", T["yv"][:], T["YV"][0::16, :], [r("YV")], [], "oV")
     for s in range(4):
         act(r("YA", s, 1024, 4), r("AA", s, TW, 8))
     dma("Y", T["yan"][:], T["YA"][0::16, :], [r("YA")], [], "oA")
     for s in range(2):
-        yt = (r("yt"), r("junk"))[s]
-        ts(yt, r("R", 2 + s, TW, 8), 4096.0, OP.mult)
-        tt(r("YR", s, 512, 2), yt, r("R", s, TW, 8), OP.add)
+        ts(r("junk", 256 * s, 256 * s + 256), r("R", 2 + s, TW, 8), 4096.0, OP.mult)
+    for s in range(2):
+        tt(r("YR", s, 512, 2), r("junk", 256 * s, 256 * s + 256), r("R", s, TW, 8), OP.add)
     dma("Y", T["yr"][:], T["YR"][:], [r("YR")], [], "oR")
+    act(r("YL"), (r("IOT"), r("AL", 0, 16)))
+    act(r("YV"), (r("IOT"), r("VT16")))
+    dma("Y", T["ya"][:], T["YL"][0::16, :], [r("YL")], [], "oL")
+    dma("Y", T["yv"][:], T["YV"][0::16, :], [r("YV")], [], "oV")
     for t in range(3):
         cp(r("YH", t, 256, 4), r("R", 4 + t, TW, 32))
     Q["V"].wait_ge(T.sem["arr3"], len(topo.engines(T.cores[(rank - 4) % N], core)))

from concourse.mybir import AluOpType as OP, ActivationFunctionType as AF, AxisListType

TW = 2048
DUMP = 3072
KV = 12
KA = 4
N1 = (0, 4, 4, 0)
W1 = 1
W0 = 0
NG = 10
PLAN = (("Vq", 0, 64), ("Vq", 64, 128), ("Vg", 128, 160), ("Sg", 192, 256), ("Q", 0, 64), ("Sg", 160, 192),
        ("D", 192, 0), ("D", 224, 1), ("A", 192, 0), ("A", 224, 1), ("M", 0, 64), ("D", 128, 0), ("K",), ("D", 160, 1),
        ("Q", 64, 128), ("M", 192, 256), ("A", 128, 0), ("A", 160, 1), ("M", 64, 128), ("M", 128, 192))
SCRATCH = {}
for _n, _w, _d in (
    ("X2", 4096, "bfloat16"), ("R", 5120, "int32"), ("AA", 5120, "float32"), ("OWB", 2048, "float32"),
    ("OWN", 1024, "float32"), ("U", 1024, "float32"), ("KN", 1024, "float32"), ("QS", 1024, "bfloat16"),
    ("IOT", 2048, "float32"), ("SXF", 4096, "float32"), ("SXS", 2048, "float32"), ("MX", 4096, "bfloat16"),
    ("QX", 2048, "bfloat16"), ("XG", 4096, "bfloat16"), ("DD", 4096, "bfloat16"), ("AD", 4096, "bfloat16"),
    ("E", 2048, "bfloat16"), ("q", 256, "bfloat16"), ("u", 256, "float32"), ("kn", 256, "float32"),
    ("ow", 256, "float32"), ("aB", 256, "float32"), ("AB", 512, "float32"), ("e", 256, "float32"),
    ("prod", 256, "int32"), ("pl", 256, "int32"), ("pl16", 256, "uint16"), ("eqs", 256, "float32"),
    ("xk", 256, "float32"), ("m", 256, "int32"), ("hit", 256, "bfloat16"), ("F", 264, "int32"),
    ("fitb", 256, "float32"), ("cum", 256, "float32"), ("junk", 1024, "float32"), ("acc", 4, "float32"),
    ("inv16", 8, "uint16"), ("QT", 256, "bfloat16"), ("wsx", 256, "float32"),
    ("fit", 16, "float32"), ("nf", 16, "float32"), ("f256", 16, "float32"), ("Aw", 32, "float32"), ("dA", 16, "float32"),
    ("tA", 16, "float32"), ("aw", 16, "float32"), ("vtw", 16, "float32"), ("vw", 16, "float32"), ("vsw", 16, "float32"),
    ("AL", 32, "uint16"), ("VT16", 16, "uint16"), ("VS16", 16, "uint16"),
    ("bsum", 1, "float32"), ("bI", 2, "int32"), ("th4", 1, "float32"), ("thb", 1, "float32"),
    ("thI", 1, "int32"), ("wI", 1, "int32"), ("wF", 1, "float32"),
    ("pI", 1, "int32"), ("pF", 1, "float32"), ("qI", 1, "int32"), ("q16", 1, "float32"), ("c15", 1, "float32"),
    ("rI", 1, "int32"), ("rF", 1, "float32"), ("hI", 1, "int32"), ("m1", 1, "float32"), ("m0", 1, "float32"),
    ("kI", 2, "int32"), ("ck", 1, "float32"),
    ("jc", 4, "float32"), ("CI", 144, "float32"), ("CB", 128, "float32"), ("C16", 16, "float32"),
    ("Z1", 144, "bfloat16"), ("Z4", 144, "bfloat16"), ("Z8", 144, "bfloat16"), ("ZW", 144, "bfloat16"), ("Z0F", 144, "float32"),
    ("BO", 128, "bfloat16"), ("BOW", 128, "bfloat16"), ("BON", 128, "bfloat16"), ("B0", 128, "float32"),
    ("ID", 128, "bfloat16"), ("NI", 128, "bfloat16"), ("IZ", 128, "float32"), ("I0", 128, "float32"),
    ("IDF", 128, "float32"), ("ONF", 144, "float32"),
    ("ON", 256, "bfloat16"), ("CSE", 128, "bfloat16"), ("CSO", 128, "bfloat16"),
    ("AC", 128, "int32"), ("OC", 128, "int32"), ("ACF", 128, "float32"), ("OCF", 128, "float32"),
    ("TI", 160, "float32"), ("TT", 160, "float32"), ("t0", 80, "float32"), ("t1", 80, "float32"), ("WW", 80, "float32"),
    ("uI", 256, "int32"), ("uA", 256, "int32"), ("uwI", 64, "int32"), ("uwA", 64, "int32"), ("uwF", 64, "float32"),
    ("pr", 64, "int32"), ("bs", 64, "int32"), ("OL", 1024, "uint16"), ("bt", 64, "int32"),
    ("YR", 512, "float32"), ("YH", 256, "float32"), ("YA", 1024, "float32"),
    ("YV", 256, "float32"), ("YL", 256, "float32"),
    ("SND", 256, "int32"), ("ARR", 256, "int32"),
):
    SCRATCH[_n] = ("sbuf", [128, _w], _d)
PS = ("pK", "pE", "pO", "pD0", "pD1", "pC", "pW")
for _n in PS:
    SCRATCH[_n] = ("psum", [128, 512], "float32")
SCRATCH["pT"] = ("psum", [128, 1024], "bfloat16")
PSUM = PS + ("pT",)
DMAS = {"lAC": 1, "lOC": 1, "lWT": 2, "lX": 1, "lXb": 1, "lR": 1, "gOW": 16, "gAA": 16, "gSF": 1, "gSX": 16,
        "oR": 1, "oH": 1, "oA": 1, "oV": 1, "oL": 1}
SEMAPHORES = ["V", "S", "P", "G", "snd"] + ["arr%d" % t for t in range(4)] + list(DMAS)


def _meet(a, b):
    if a[0] >= b[1] or b[0] >= a[1]:
        return False
    if a[2] == b[2]:
        return a[2] == 1 or (a[0] - b[0]) % a[2] == 0
    if a[2] == 1 or b[2] == 1:
        if b[2] == 1:
            a, b = b, a
        first = b[0] + max(0, -((b[0] - a[0]) // b[2])) * b[2]
        return first < min(a[1], b[1])
    return True


def _covers(a, b):
    return a == b or (a[2] == 1 and a[0] <= b[0] and a[1] >= b[1])


def rank_program(g, core, T, topo):
    rank = T.rank_of(core)
    if rank is None:
        return
    N = len(T.cores)
    Q = {"V": g.vector, "S": g.scalar, "P": g.tensor, "G": g, "Y": g.sync}
    count = {k: 0 for k in "VSPG"}
    known = {k: {} for k in Q}
    log = {}

    def r(name, lo=0, hi=None, st=1):
        return (name, lo, SCRATCH[name][1][1] if hi is None else hi, st)

    def ap(x):
        if len(x) == 2:
            return ap(x[0]).indirect(ap(x[1]))
        n, lo, hi, st = x
        return T[n][:, lo:hi:st] if st > 1 else T[n][:, lo:hi]

    def flat(xs):
        out = []
        for x in xs:
            if isinstance(x, tuple):
                if len(x) == 2:
                    out += [x[0], x[1]]
                else:
                    out.append(x)
        return out

    def learn(eng, sem, val, clock):
        kn = known[eng]
        if kn.get(sem, 0) >= val:
            return
        Q[eng].wait_ge(T.sem[sem], val)
        for s, x in clock.items():
            if kn.get(s, 0) < x:
                kn[s] = x
        kn[sem] = max(kn.get(sem, 0), val)

    def op(eng, fn, reads, writes, grp=None):
        reads, writes = flat(reads), flat(writes)
        need = {}
        for acc, wr in [(x, False) for x in reads] + [(x, True) for x in writes]:
            bank = acc[0] in PSUM
            for (sp, w2, eng2, sem, val, clock, grp2) in log.get(acc[0], ()):
                if grp is not None and grp2 == grp:
                    continue
                if eng2 == eng and grp2 is None and grp is None:
                    if (bank and eng == "P") or not (wr or w2) or not _meet(acc[1:], sp):
                        continue
                elif bank:
                    pass
                else:
                    if not (wr or w2) or not _meet(acc[1:], sp):
                        continue
                if sem not in need or need[sem][0] < val:
                    need[sem] = (val, clock)
        for sem in sorted(need, key=lambda s: -len(need[s][1])):
            learn(eng, sem, need[sem][0], need[sem][1])
        ins = fn()
        if grp is None:
            count[eng] += 1
            sem, val = eng, count[eng]
            ins.then_inc(T.sem[sem], 1)
        else:
            sem, val = grp, 16 * DMAS[grp]
            ins.then_inc(T.sem[sem], 16)
        clock = dict(known[eng])
        clock[sem] = val
        for acc, wr in [(x, False) for x in reads] + [(x, True) for x in writes]:
            old = log.setdefault(acc[0], [])
            keep = []
            for rec in old:
                gone = False
                if grp is None or rec[6] != grp:
                    if wr and _covers(acc[1:], rec[0]):
                        gone = True
                    elif not wr and not rec[1] and rec[2] == eng and rec[6] is None and grp is None and _covers(acc[1:], rec[0]):
                        gone = True
                if not gone:
                    keep.append(rec)
            keep.append((acc[1:], wr, eng, sem, val, clock, grp))
            log[acc[0]] = keep

    def sc(x):
        return ap(x) if isinstance(x, tuple) else x

    def tt(o, a, b, f):
        op("V", lambda: g.vector.tensor_tensor(out=ap(o), in0=ap(a), in1=ap(b), op=f), [a, b], [o])

    def ts(o, a, s1, f, s2=None, f2=None):
        if f2 is None:
            op("V", lambda: g.vector.tensor_scalar(out=ap(o), in0=ap(a), scalar1=sc(s1), scalar2=None, op0=f), [a, s1], [o])
        else:
            op("V", lambda: g.vector.tensor_scalar(out=ap(o), in0=ap(a), scalar1=sc(s1), scalar2=sc(s2), op0=f, op1=f2), [a, s1, s2], [o])

    def cp(o, a):
        op("V", lambda: g.vector.tensor_copy(out=ap(o), in_=ap(a)), [a], [o])

    def scatter(win, off, a):
        op("V", lambda: g.vector.tensor_copy(out=ap((win, off)), in_=ap(a)), [a, off], [win])

    def act(o, a, f=AF.Copy, bias=None, scale=None, acc=None):
        kw = {}
        if bias is not None:
            kw["bias"] = sc(bias)
        if scale is not None:
            kw["scale"] = sc(scale)
        if acc is not None:
            kw["accum_out"] = ap(acc)
        op("S", lambda: g.scalar.activation(out=ap(o), in_=ap(a), func=f, **kw), [a, bias, scale], [o] + ([acc] if acc else []))

    def mm(o, l, x, start, stop):
        op("P", lambda: g.tensor.matmul(out=ap(o), lhsT=ap(l), rhs=ap(x), start=start, stop=stop), [l, x], [o])

    def dma(eng, out, in_, reads, writes, grp):
        op(eng, lambda: Q[eng].dma_start(out=out, in_=in_), reads, writes, grp)

    def iota(o, pattern, cm, base=0):
        op("G", lambda: g.iota(ap(o), pattern, base, cm, allow_small_or_imprecise_dtypes=True), [], [o])

    def sel(o, a, pattern, cmp, base, cm):
        op("G", lambda: g.affine_select(ap(o), ap(a), pattern, cmp, 0.0, base, cm), [a], [o])

    def Z(name, k):
        return r(name, 15 - k, 143 - k)

    dma("Y", T["AC"][:], T["an"][:], [], [r("AC")], "lAC")
    dma("S", T["X2"][:, 0:TW], T["xc"][:], [], [r("X2", 0, TW)], "lX")
    dma("Y", T["OC"][:], T["rf"][0::16, :], [], [r("OC")], "lOC")
    dma("Y", T["wI"][:], T["w"][:], [], [r("wI")], "lWT")
    dma("Y", T["thI"][:], T["th"][:], [], [r("thI")], "lWT")
    dma("S", T["X2"][:, TW:2 * TW], T["xc"][:], [], [r("X2", TW, 2 * TW)], "lXb")
    dma("Y", T["R"][:, 0:TW], T["rf"][:], [], [r("R", 0, TW)], "lR")

    iota(r("pI"), [[1, 1]], 1)
    iota(r("CB"), [[16, 8], [0, 16]], 0)
    iota(r("CI"), [[1, 144]], 0)
    iota(r("C16"), [[16, 16]], 0)
    for name, c in (("ON", 1), ("CSO", -3 * (1 << 16)), ("CSE", -(1 << 17)), ("ONF", 1)):
        iota(r(name), [[0, SCRATCH[name][1][1]]], 0, c)
    cp(r("pF"), r("pI"))
    ts(r("qI"), r("pI"), 112, OP.bitwise_and)
    ts(r("rI"), r("pI"), 15, OP.bitwise_and)
    ts(r("hI"), r("pI"), 4, OP.arith_shift_right, 1, OP.bitwise_and)
    cp(r("q16"), r("qI"))
    cp(r("rF"), r("rI"))
    cp(r("m1"), r("hI"))
    ts(r("c15"), r("qI"), 15.0, OP.add)
    CI, C128 = r("CI"), r("CI", 0, 128)
    ts(r("BON"), r("CB"), r("q16"), OP.is_equal, -4096.0, OP.mult)
    sel(r("BON"), r("BON"), [[0, 8], [-1, 16]], OP.is_ge, KV - 1, 0)
    O8 = r("ONF", 0, 128)
    sel(r("IZ"), O8, [[-1, 128]], OP.is_equal, 0, 1)
    sel(r("IZ"), r("IZ"), [[0, 8], [1, 16]], OP.not_equal, 0, 0)
    sel(r("B0"), O8, [[-16, 8], [0, 16]], OP.is_equal, 0, 1)
    sel(r("I0"), O8, [[-16, 8], [-1000, 16]], OP.is_equal, 0, 1)
    sel(r("IDF"), O8, [[-1, 128]], OP.is_equal, 0, 1)
    ts(r("m0"), r("m1"), 0.0, OP.is_equal)
    ts(r("kI", 0, 1), r("rI"), 613.0, OP.mult)
    ts(r("vtw"), r("C16"), r("rF"), OP.add)
    ts(r("kI", 1, 2), r("kI", 0, 1), 2047, OP.bitwise_and)
    for c in range(4):
        ts(r("jc", c, c + 1), r("rF"), 16.0 * c + 0.5, OP.add)
    ts(r("vw"), r("vtw"), 8.0, OP.mult)
    cp(r("ck"), r("kI", 1, 2))
    ts(r("AL", 16, 32), r("vtw"), float(TW), OP.add)
    cp(r("OCF"), r("OC"))
    cp(r("ACF"), r("AC"))
    cp(r("wF"), r("wI"))
    for s in range(4):
        for h in range(2):
            act(r("TI", 32 + 32 * s + 16 * h, 48 + 32 * s + 16 * h), r("OCF", s, 128, 8))
    ts(r("ZW"), CI, r("c15"), OP.is_equal, r("wF"), OP.mult)
    ts(r("BOW"), r("CB"), r("q16"), OP.is_equal, r("wF"), OP.mult)
    for h in range(2):
        act(r("TI", 16 * h, 16 * h + 16), r("ACF", 0, 128, 8))
    ts(r("ID"), C128, r("pF"), OP.is_equal)
    op("V", lambda: g.vector.transpose(out=ap(r("TT")), in_=ap(r("TI"))), [r("TI")], [r("TT")])
    ts(r("NI"), C128, r("pF"), OP.is_equal, -1.0, OP.mult)
    for n in range(5):
        sl = (16 * n, 16 * n + 16)
        act(r("t0", *sl), r("TT", 32 * n, 32 * n + 16), AF.Copy, scale=r("m0"))
        ts(r("t1", *sl), r("TT", 32 * n + 16, 32 * n + 32), r("m1"), OP.mult)
    tt(r("WW"), r("t0"), r("t1"), OP.add)
    ts(r("Z4"), CI, r("c15"), OP.is_equal, 4096.0, OP.mult)
    cp(r("AL", 0, 16), r("WW", 0, 16))
    for p in range(16):
        dma("Y", T["OWB"][p::16, :], T["OCF"][:], [r("OCF")], [r("OWB")], "gOW")
    for p in range(16):
        dma("Y", T["AA"][p::16, 0:TW], T["ACF"][:], [r("ACF")], [r("AA", 0, TW)], "gAA")
    for k in range(16):
        sel(r("E", k, 2048, 16), r("NI"), [[0, 128]], OP.is_equal, 0, 0)
    sel(r("Z0F"), r("ONF"), [[16, 9], [1000, 16]], OP.is_equal, -15000, -1)
    for o in ("BO", "Z1"):
        w, x = (128, 0) if o == "BO" else (144, 1000)
        sel(r(o), r("ON", 0, w), [[-16, w // 16], [x, 16]], OP.is_ge, -15 * x, 1)
        sel(r(o), r(o), [[16, w // 16], [0, 16]], OP.is_ge, 15, -1)
    iota(r("IOT"), [[1, 2048]], 0)

    def uw_p(s):
        for p in range(16):
            mm(r("pW", 64 + 16 * s, 80 + 16 * s), Z("ZW", p), r("X2", 8 * p + s, TW, 128), p == 0, p == 15)

    def lists(lo, hi):
        a, b = 16 * lo, 16 * hi
        cp(r("uwI", a, b), r("pW", 64 + a, 64 + b))
        ts(r("uwA", a, b), r("uwI", a, b), 4095, OP.bitwise_and)
        ts(r("uwF", a, b), r("uwA", a, b), 32.0, OP.add)
        tt(r("pr", a, b), r("uwF", a, b), r("WW", 16 + a, 16 + b), OP.mult)
        ts(r("bs", a, b), r("pr", a, b), 5, OP.arith_shift_right, 2047, OP.bitwise_and)
        for k in list(range(KV, 16)) + list(range(KV)):
            ts(r("OL", 64 * k + a, 64 * k + b), r("bs", a, b), float(613 * k % TW), OP.add)

    def utab_p(s):
        mm(r("pC", 0, 256), r("BOW"), r("X2", s, TW, 8), True, True)

    def utab_v(s):
        cp(r("uI"), r("pC", 0, 256))
        ts(r("uA"), r("uI"), 4095, OP.bitwise_and)
        ts(r("U", 256 * s, 256 * s + 256), r("uA"), 32.0, OP.add)

    def qs(s):
        act(r("QS", 256 * s, 256 * s + 256), r("X2", s, TW, 8))

    def own_v(s, ks):
        for k in ks:
            tt(r("MX", 256 * k, 256 * k + 256), (r("X2"), r("OL", 64 * k + 16 * s, 64 * k + 16 * s + 16)),
               r("QS", 256 * s, 256 * s + 256), OP.max)

    SA, SB = list(range(KV, KV + KA)), list(range(KV + KA, 16))

    def own_sg(s, ks):
        for k in ks:
            act(r("XG", 256 * (k - KV), 256 * (k - KV) + 256), (r("X2"), r("OL", 64 * k + 16 * s, 64 * k + 16 * s + 16)))

    def own_sd(s, ks):
        for k in ks[::2]:
            b = "pD%d" % (k // 2 % 2)
            mm(r(b), r("ID"), r("XG", 256 * (k - KV), 256 * (k - KV) + 512), True, False)
            for h in range(2):
                mm(r(b, 256 * h, 256 * h + 256), r("NI"), r("QS", 256 * s, 256 * s + 256), False, h == 1)

    def own_sa(ks):
        for k in ks[::2]:
            act(r("MX", 256 * k, 256 * k + 512), r("pD%d" % (k // 2 % 2)), AF.Abs)

    def own_p(s, ks, first=False, last=False):
        o = r("pO", 0, 256)
        if first:
            mm(o, r("CSO"), r("ON"), True, False)
            mm(o, r("BON"), r("QS", 256 * s, 256 * s + 256), False, False)
        ks = list(ks)
        for k in ks:
            mm(o, Z("Z8" if k < KV else "Z4", k), r("MX", 256 * k, 256 * k + 256), False, last and k == ks[-1])

    def own_w(s):
        tt(r("wsx"), (r("SXS"), r("OL", 16 * s, 16 * s + 16)), r("OWB", s, TW, 8), OP.add)

    def own_k(s):
        tt(r("KN", 256 * s, 256 * s + 256), r("wsx"), r("pO", 0, 256), OP.add)

    def wrap():
        for p in range(16):
            mm(r("pW", 0, 32), Z("Z0F", p), r("AB", p, 512, 16), p == 0, p == 15)

    HALVES = sorted({x[1] // 128 for x in PLAN if x[0] == "D"})
    NQ = sum(x[2] - x[1] for x in PLAN if x[0] == "Vq")

    def turn(q):
        for h in HALVES:
            src = (q[0], q[1] + 128 * h, q[1] + 128 * h + 128, 1)
            op("P", lambda: g.tensor.transpose(out=ap(r("pT", 128 * h, 128 * h + 128)), in_=ap(src), identity=ap(r("ID"))),
               [src, r("ID")], [r("pT", 128 * h, 128 * h + 128)])
        a, b = 128 * HALVES[0], 128 * HALVES[-1] + 128
        act(r("QT", a, b), r("pT", a, b))

    def spread(q, ng):
        src = (q[0], q[1], q[1] + NQ, 1)
        for k in range(16):
            if k < 16 - ng:
                act(r("QX", k, 16 * NQ, 16), src)
            else:
                sel(r("QX", k, 16 * NQ, 16), src, [[0, NQ]], OP.is_equal, 0, 0)

    uw_p(0)
    utab_p(0)
    qs(0)
    lists(0, 1)
    utab_v(0)
    turn(r("QS", 0, 256))
    spread(r("QS", 0, 256), 0)
    for c in range(4):
        b = "pD%d" % (c % 2)
        mm(r(b), r("BON"), r("X2", 512 * c, 512 * c + 512), True, True)
        act(r("SXF", 512 * c, 512 * c + 512), r(b), AF.Identity, bias=float(4096 * 2048 + 2048))
    dma("Y", T["SXF"][:, TW:2 * TW], T["SXF"][:, 0:TW], [r("SXF", 0, TW)], [r("SXF", TW, 2 * TW)], "gSF")
    for k in range(16):
        d = 613 * k % TW
        dma("Y", T["SXS"][k::16, :], T["SXF"][k::16, d:d + TW], [r("SXF")], [r("SXS")], "gSX")
    own_v(0, range(0, W0))
    for s in range(1, 4):
        uw_p(s)

    for t in range(4):
        if t == 0:
            u, kn, ow = r("U", 0, 256), r("KN", 0, 256), r("OWB", 0, TW, 8)
        else:
            u, kn, ow = r("pE", 0, 256), r("pW", 128, 384), r("ow")
            a, b = 64 * (t - 1), 64 * t
            Q["V"].wait_ge(T.sem["arr%d" % (t - 1)], len(topo.engines(T.cores[(rank - t) % N], core)))
            tt(r("bt"), r("ARR", a, b), r("R", 4 + t - 1, TW, 32), OP.max)
            ts(r("R", 4 + t - 1, TW, 32), r("bt"), 2047, OP.bitwise_and)
        cp(r("e"), (r("R", 0, TW), r("AL", 0, 16)))
        tt(r("prod"), r("e"), u, OP.mult)
        ts(r("pl"), r("prod"), 5, OP.arith_shift_right, 2047, OP.bitwise_and)
        ts(r("pl16"), r("pl"), r("ck"), OP.add)
        if t < 3:
            utab_p(t + 1)
        Ke = r("pK", 0, 256)
        mm(Ke, r("CSE"), r("ON"), True, False)
        mm(Ke, r("I0"), ow, False, False)
        mm(Ke, r("IZ"), r("e"), False, False)
        mm(r("pE", 0, 256), r("B0"), r("e"), True, True)
        lastm = [x for x in PLAN if x[0] == "M"][-1]
        for x in PLAN:
            if x[0] == "Vq":
                lo, hi = x[1:]
                tt(r("DD", 16 * lo, 16 * hi), (r("X2"), r("pl16", lo, hi)), r("QX", 16 * lo, 16 * hi), OP.subtract)
            elif x[0] == "Vg":
                lo, hi = x[1:]
                cp(r("XG", 16 * lo, 16 * hi), (r("X2"), r("pl16", lo, hi)))
            elif x[0] == "Sg":
                lo, hi = x[1:]
                act(r("XG", 16 * lo, 16 * hi), (r("X2"), r("pl16", lo, hi)))
            elif x[0] == "Q":
                lo, hi = x[1:]
                act(r("AD", 16 * lo, 16 * hi), r("DD", 16 * lo, 16 * hi), AF.Abs)
            elif x[0] == "D":
                lo, b, h = x[1], "pD%d" % x[2], x[1] // 128
                mm(r(b), r("ID"), r("XG", 16 * lo, 16 * lo + 512), True, False)
                mm(r(b), r("QT", 128 * h, 128 * h + 128), r("E", 16 * (lo - 128 * h), 16 * (lo - 128 * h) + 512), False, True)
            elif x[0] == "A":
                act(r("AD", 16 * x[1], 16 * x[1] + 512), r("pD%d" % x[2]), AF.Abs)
            elif x[0] == "M":
                lo, hi = x[1:]
                for k in range(16):
                    mm(r("pK", lo, hi), Z("Z4", k), r("AD", 16 * lo + k, 16 * hi, 16), False, x is lastm and k == 15)
            elif t > 0:
                own_w(t)
                own_k(t)
                act(r("kn"), (r("KN", 0, 256 * (t + 1)), r("VT16")))
                mm(kn, r("IDF"), r("kn"), True, True)
        if t == 0:
            ts(r("Z8"), CI, r("c15"), OP.is_equal, 8192.0, OP.mult)
            op("V", lambda: g.vector.memset(ap(r("F", 256, 264)), -4096), [], [r("F", 256, 264)])
            ts(r("th4"), r("thI"), 4096.0, OP.mult, -float(1 << 24), OP.add)
            own_v(0, range(W0, KV))
            act(r("AA", TW, TW + 256), r("AA", 1, TW, 8))
            act(r("AB"), (r("AA", 0, TW + 256), r("AL")))
            wrap()
            own_sg(0, SA + SB)
            own_p(0, range(KV), True)
            own_sd(0, SA + SB)
            own_sa(SA + SB)
            own_p(0, SA + SB, False, True)
        if t < 3:
            utab_v(t + 1)
        tt(r("eqs"), r("e"), r("pE", 0, 256), OP.is_equal)
        if t == 0:
            own_w(0)
            lists(1, 4)
            own_k(0)
            for s in range(1, 4):
                qs(s)
                act(r("AA", TW + 256 * s, TW + 256 * s + 256), r("AA", s + 1, TW, 8))
            act(r("aB"), (r("IOT"), r("AL", 0, 16)))
        tt(r("xk"), r("eqs"), kn, OP.mult)
        cp(r("Aw"), r("pW", 0, 32))
        tt(r("dA"), r("Aw", 16, 32), r("Aw", 0, 16), OP.subtract)
        n1 = N1[t]
        if t < 3:
            own_v(t + 1, range(0, n1))
            own_sg(t + 1, SA)
        tt(r("m"), r("xk"), Ke, OP.min)
        ts(r("hit"), r("m"), r("th4") if t == 0 else r("thb"), OP.is_lt)
        mm(r("pC", 0, 256), r("BO"), r("hit"), True, True)
        cw = r("pE", 256, 272)
        for p in range(16):
            mm(cw, Z("Z1", p), r("hit", p, 256, 16), p == 0, p == 15)
        ts(r("F", 0, 256), r("m"), 2047, OP.bitwise_and)
        ts(r("fitb"), r("pC", 0, 256), 7.5, OP.is_ge)
        op("V", lambda: g.vector.tensor_tensor_scan(ap(r("cum")), ap(r("fitb")), ap(r("fitb")), 0.0, OP.add, OP.max),
           [r("fitb")], [r("cum")])
        for c in range(4):
            act(r("junk", 256 * c, 256 * c + 256), r("cum"), AF.Sign, bias=r("jc", c, c + 1), scale=-1.0, acc=r("acc", c, c + 1))
        ts(r("fit"), cw, 7.5, OP.is_ge)
        ts(r("nf"), cw, 7.5, OP.is_lt, float(DUMP), OP.mult)
        if t < 3:
            ts(r("f256"), cw, 7.5, OP.is_ge, 256.0, OP.mult)
        tt(r("tA"), r("fit"), r("dA"), OP.mult)
        tt(r("vsw"), r("vw"), r("nf"), OP.add)
        if t < 3:
            tt(r("vtw"), r("vtw"), r("f256"), OP.add)
        tt(r("aw"), r("tA"), r("Aw", 0, 16), OP.add)
        tt(r("vw"), r("vw"), r("fit"), OP.add)
        if t < 3:
            cp(r("VT16"), r("vtw"))
            ts(r("AL", 16, 32), r("vtw"), float(TW), OP.add)
        cp(r("AL", 0, 16), r("aw"))
        cp(r("VS16"), r("vsw"))
        if t < 3:
            own_sd(t + 1, SA)
            own_sa(SA)
            own_v(t + 1, range(n1, n1 + W1))
        else:
            scatter(r("AA"), r("VS16"), r("aB"))
        ts(r("inv16", 0, 4), r("acc"), 0.5, OP.mult, 128.0, OP.add)
        snd = r("SND", 64 * t, 64 * t + 64)
        ts(snd, (r("F"), r("inv16", 0, 4)), 4096.0, OP.add)
        dst = T.cores[(rank + 1 + t % (N - 1)) % N]
        rid, pid = topo.addr(dst, core)
        last = log["SND"][-1]
        learn("G", "V", last[4], last[5])
        g.remote_dma(ap(r("ARR", 64 * t, 64 * t + 64)), ap(snd), T.sem["arr%d" % t], T.sem["snd"], pid, rid, topo.mask(core, dst))
        if t < 3:
            mm(r("pE", 288, 304), r("ONF", 0, 128), r("fit"), True, True)
            scatter(r("AA"), r("VS16"), r("aB"))
            op("V", lambda: g.vector.tensor_reduce(ap(r("bsum")), ap(r("pE", 288, 304)), AxisListType.X, OP.add),
               [r("pE", 288, 304)], [r("bsum")])
        scatter(r("R"), r("VS16"), r("F", 0, 256))
        if t < 3:
            s, n = t + 1, 256 * (t + 2)
            act(r("q"), (r("QS", 0, n), r("VT16")))
            turn(r("q"))
            act(r("u"), (r("U", 0, n), r("VT16")))
            mm(r("pE", 0, 256), r("IDF"), r("u"), True, True)
            if t == 0:
                for c in range(4):
                    act(r("OWN", 256 * c, 256 * c + 256), r("OWB", c, TW, 8))
            act(r("AB"), (r("AA", 0, TW + n), r("AL")))
            own_p(s, list(range(0, n1 + W1)) + SA, True)
            spread(r("q"), NG)
            own_sg(s, SB)
            own_sd(s, SB)
            wrap()
            act(r("ow"), (r("OWN", 0, n), r("VT16")))
            own_sa(SB)
            act(r("aB"), (r("IOT"), r("AL", 0, 16)))
            own_v(s, range(n1 + W1, n1 + W1 + 1))
            cp(r("bI", 0, 1), r("bsum"))
            own_v(s, range(n1 + W1 + 1, n1 + W1 + 2))
            ts(r("bI", 1, 2), r("bI", 0, 1), 255, OP.bitwise_and)
            own_v(s, range(n1 + W1 + 2, KV))
            ts(r("thb"), r("bI", 1, 2), 4096.0, OP.mult, r("th4"), OP.add)
            own_p(s, SB + list(range(n1 + W1, KV)), False, True)

    cp(r("VT16"), r("vw"))
    for s in range(4):
        act(r("YA", s, 1024, 4), r("AA", s, TW, 8))
    dma("Y", T["yan"][:], T["YA"][0::16, :], [r("YA")], [], "oA")
    for s in range(2):
        ts(r("junk", 256 * s, 256 * s + 256), r("R", 2 + s, TW, 8), 4096.0, OP.mult)
    for s in range(2):
        tt(r("YR", s, 512, 2), r("junk", 256 * s, 256 * s + 256), r("R", s, TW, 8), OP.add)
    dma("Y", T["yr"][:], T["YR"][:], [r("YR")], [], "oR")
    act(r("YL"), (r("IOT"), r("AL", 0, 16)))
    act(r("YV"), (r("IOT"), r("VT16")))
    dma("Y", T["ya"][:], T["YL"][0::16, :], [r("YL")], [], "oL")
    dma("Y", T["yv"][:], T["YV"][0::16, :], [r("YV")], [], "oV")
    for t in range(3):
        cp(r("YH", t, 256, 4), r("R", 4 + t, TW, 32))
    Q["V"].wait_ge(T.sem["arr3"], len(topo.engines(T.cores[(rank - 4) % N], core)))
    tt(r("bt"), r("ARR", 192, 256), r("R", 7, TW, 32), OP.max)
    ts(r("R", 7, TW, 32), r("bt"), 2047, OP.bitwise_and)
    cp(r("YH", 3, 256, 4), r("R", 7, TW, 32))
    dma("Y", T["yh"][:], T["YH"][:], [r("YH")], [], "oH")
    for grp in DMAS:
        g.wait_ge(T.sem[grp], 16 * DMAS[grp])
    for e in "VSPG":
        g.wait_ge(T.sem[e], count[e])
    g.wait_ge(T.sem["snd"], sum(len(topo.engines(core, T.cores[(rank + 1 + t) % N])) for t in range(4)))
